import numpy as np, ml_dtypes
CORES = [5,29,101,125,133,157,229,253]
N = 8
import mx_ref
BF = ml_dtypes.bfloat16
def gentries(a):
    return np.ascontiguousarray(a.reshape(8, 16, -1).transpose(0, 2, 1)).reshape(8, -1)
def gtable(e):
    e = np.asarray(e); return np.ascontiguousarray(e.reshape(8, -1, 16).transpose(0, 2, 1)).reshape(128, -1).astype(np.int32)
def gcols(t, e):
    v = np.concatenate([t.reshape(8, 16, -1, 4), np.zeros((8, 16, 1, 4), BF)], axis=2)
    return np.ascontiguousarray(np.stack([v[g][:, e[g]] for g in range(8)])).reshape(128, -1)
def tile(rs):
    return np.stack(rs, axis=2).reshape(128, -1).astype(BF)
def pick(q, e):
    c = np.concatenate([q[0].reshape(128, -1, 4), np.zeros((128, 1, 4), np.uint8)], axis=1); s = np.concatenate([q[1], np.ones((16, 1), np.uint8)], axis=1)
    return (np.ascontiguousarray(c[:, e].reshape(128, -1)), np.ascontiguousarray(s[:, e]))
def join(*qs):
    return (np.concatenate([q[0] for q in qs], axis=1), np.concatenate([q[1] for q in qs], axis=1))
def put(q, e, v):
    c, s = q[0].reshape(128, -1, 4).copy(), q[1].copy(); c[:, e] = v[0].reshape(128, -1, 4); s[:, e] = v[1]
    return (c.reshape(128, -1), s)
def pk(c, s):
    return (np.ascontiguousarray(c), mx_ref.live(s))
def emit(q):
    return q[0], q[1]
def packed(v, rng):
    q = [mx_ref.quantize(np.ascontiguousarray(v[r])) for r in range(N)]
    return np.stack([a for a, b in q]), np.stack([mx_ref.plane(b, rng) for a, b in q])
def values_of_codes():
    e, c = np.zeros((128, 128, 4), np.float32), np.zeros((128, 2, 4), np.uint8)
    e[np.arange(128), np.arange(128), 0] = 1
    c[:127, :, 0] = np.arange(256).reshape(2, 128).T[:127]
    return mx_ref.matmul(mx_ref.quantize(e.reshape(128, 512).astype(BF)), (c.reshape(128, 8), np.full((16, 2), 127, np.uint8))).T.reshape(-1).astype(np.float64)
CODE_VALUE, SCALE_VALUE = values_of_codes(), 2.0 ** (np.arange(256) - 127.0)
def decode(q):
    return (CODE_VALUE[q[0]].reshape(16, 8, -1, 4) * SCALE_VALUE[q[1]][:, None, :, None] + 0.0).reshape(128, -1).astype(np.float32)
def f(rng, *shape):
    return mx_ref.flush((rng.standard_normal(shape, dtype=np.float32) * np.exp2(rng.integers(-2, 3, shape[:-1] + (1,)))).astype(BF))
def wide(rng, *shape, cols=0):
    v = rng.standard_normal(shape, dtype=np.float32) * np.exp2(rng.integers(-12, 13, shape)).astype(np.float32)
    if cols: v *= np.repeat(np.exp2(rng.integers(-cols, cols + 1, shape[:-2] + (1, shape[-1] // 4))) * (rng.random(shape[:-2] + (1, shape[-1] // 4)) > 0.0625), 4, axis=-1).astype(np.float32)
    return mx_ref.flush(v.astype(BF))
C, K, R = 288, 160, 3
def numbers_of(rng):
    return np.array(f(rng, N, 128, 4 * C)), np.array(f(rng, N, 128, 512)), np.array(f(rng, N, 128, 512))
def operands(rng):
    return rng.integers(0, C, (N, 8, C))
def layers(rng, still=[]):
    w = np.array(f(rng, N, 128, 2048)).reshape(N, 8, 16, 4, 8, 16, 4)
    for i in still:
        w[:, :, i] = 0
        w[:, :, :, :, :, i] = 0
    return w
def clear(u):
    a = u.reshape(N, 128, 128, 4)
    for i in range(5): a[:, :, i::16] = 0
    return a
def given(rng, x, l, m, u, v, w):
    c, s = packed(np.ascontiguousarray(w).reshape(N, 128, 2048), rng)
    return {"x": x.reshape(N, 128, 4 * C).astype(BF), "l": np.stack([gtable(l[r]) for r in range(N)]), "m": np.stack([gtable(m[r]) for r in range(N)]), "u": u.reshape(N, 128, 512), "v": v, "wc": c, "ws": s}
def setup_inputs(rng):
    x, u, v = numbers_of(rng)
    return given(rng, x, operands(rng), operands(rng), u, v, layers(rng))
def setup_inputs_ties(rng):
    x, u, v = numbers_of(rng)
    x = x.reshape(N, 8, 16, C, 4)
    x[:, :, 0] = 0
    x[:, :, 0, :, 0] = np.exp2(rng.integers(0, 3, (N, 8, C))).astype(BF)
    x[:, :, 1] = rng.integers(-1, 2, (N, 8, C, 4)).astype(np.float32).astype(BF)
    a = clear(u)
    o = rng.permutation(N)
    for r in range(N):
        for h in range(0, 128, 16):
            a[r, h, h, 0] = 0.0 if r == o[0] else -1.0 if r == o[1] else 1.0
            for b in range(4): a[r, h + 1, h + 1 + b, b] = 1.0
    e = o[2]
    x[e, :, 8:] = 0
    x[e, :, 8, :, 0] = 1.96875
    for i in range(6):
        x[e, :, 9 + i, :, 0] = ((1 + 0.125 * rng.integers(0, 8, (8, C))) * 2.0 ** -(10 + i)).astype(np.float32).astype(BF)
        for h in range(0, 128, 16):
            a[e, h, h, 0] = 0.0
            a[e, h + 9 + i, h, 0] = 2.0 ** (10 + i)
    return given(rng, x, operands(rng), operands(rng), a, v, layers(rng, [0, 1, 8, 9, 10, 11, 12, 13, 14, 15]))
def setup_inputs_near(rng):
    x, u, v = numbers_of(rng)
    x = x.astype(np.float32).reshape(N, 8, 16, C, 4)
    x[:, :, 0] = 0
    x[:, :, 8:] = 0
    a = clear(u)
    o = rng.permutation(N) % 4
    for r in range(N):
        if o[r] < 3:
            s = rng.integers(0, 16, (8, C))
            x[r, :, 8] = ((s[:, :, None] >> np.arange(4)) & 1) * np.exp2(np.arange(4) - 23.0)
            x[r, :, 12] = rng.integers(-1, 2, (8, C, 4)) * 2.0 ** -16
        else:
            x[r, :, 10] = rng.integers(-1, 2, (8, C, 4)) * 2.0 ** -29
            x[r, :, 12, :, :2] = (rng.integers(0, 2, (8, C, 2)) * 2.0 - 1.0) * 2.0 ** -30
            x[r, :, 12, :, 2:] = rng.integers(-1, 2, (8, C, 2)) * 2.0 ** -29
        if o[r] < 2:
            x[r, :, 0, :, 0] = rng.integers(0, 2, (8, C)) * 2.0 - 1.0 if o[r] == 0 else -1.0
            x[r, :, 11, :, 0] = 2.0 ** -10
        for g in rng.permutation(8)[:4]:
            c = rng.integers(C)
            x[r, g, 8:, c] = 0
            x[r, g, 0, c, 0] = 2.0 ** 29 * rng.choice([-1.0, 1.0])
            x[r, g, 12, c] = 2.0 ** 29 * rng.choice([-1.0, 1.0], 4)
        k = 1.0 if o[r] == 0 else 2.0 ** -30
        for h in range(0, 128, 16):
            a[r, h, h, 0] = k
            if o[r] < 3:
                a[r, h + 8, h] = k
                a[r, h + 11, h, 0] = k
            else: a[r, h + 10, h] = (np.array([1.0, 1.125, 1.25, 1.5]) * k).astype(BF)
            for b in range(4): a[r, h + 12, h + 1 + b, b] = k
    return given(rng, x, operands(rng), operands(rng), a, v, layers(rng, [0, 8, 9, 10, 11, 12, 13, 14, 15]))
def setup_inputs_late(rng):
    x, u, v = numbers_of(rng)
    x = x.reshape(N, 8, 16, C, 4)
    x[:, :, 0] = (rng.permutation(N) % 2 * 2.0 - 1.0).astype(BF)[:, None, None, None]
    a = clear(u)
    for h in range(0, 128, 16):
        a[:, h, h] = 1.0
        for b in range(4): a[:, h, h + 1 + b, b] = 1.0
    return given(rng, x, operands(rng), operands(rng), a, v, layers(rng))
def setup_inputs_huge(rng):
    x, u, v = numbers_of(rng)
    o = rng.permutation(N)
    c = np.where(np.argsort(rng.random((N, C)), axis=1) < C // 4, 1.0, -1.0)[:, None, None, :, None] * 2.0 ** 30
    x = (0.6 + 0.09 * rng.random((N, 8, 16, C, 4))) * c
    x[o == 0] = (0.9375 + 0.0625 * rng.integers(0, 2, (1, 8, 16, C, 4))) * c[o == 0]
    a = 2.0 ** 30 * (1.0 - 0.1 * rng.random((N, 128, 8, 4)))
    a[o == 0] = 2.0 ** 30
    for r in range(N): a[r] *= (rng.permutation(8) % 2 * 2.0 - 1.0)[None, :, None]
    u = u.reshape(N, 128, 128, 4)
    u[:, :, ::16] = a.astype(np.float32).astype(BF)
    w = np.zeros((N, 128, 4, 128, 4), np.float32)
    i = np.arange(128)
    for b in range(4): w[:, i, b, i, b] = -2
    return given(rng, x.astype(np.float32), operands(rng), operands(rng), u, v, w.astype(BF))
def setup_inputs_spread(rng):
    x, u, v = numbers_of(rng)
    x = np.array(wide(rng, N, 128, 4 * C, cols=6)).reshape(N, 16, 8, C, 4)
    t = np.exp2(-rng.integers(8, 15, (N, 16, 8, C // 8, 4)).astype(np.float64)) * (1 + (2 * rng.integers(0, 64, (N, 16, 8, C // 8, 4)) + 1) * 2.0 ** -7)
    t[:, :, 0, :, 0] = 1.96875
    x[:, :, :, 3::8] = (t * rng.choice([-1.0, 1.0], t.shape)).astype(np.float32).astype(BF)
    l, m = 2 * rng.integers(0, C // 2, (N, 8, C)), 2 * rng.integers(0, C // 2, (N, 8, C))
    e = rng.permutation(N)
    l[e[0]], m[e[0]] = C - 1, 0
    l[e[1]] = m[e[1]]
    l[e[2]], m[e[2]] = np.arange(C), C - 1 - np.arange(C)
    l[e[3]], m[e[3]] = rng.integers(0, 2, (8, C)), rng.integers(0, 2, (8, C))
    return given(rng, x, l, m, u, v, layers(rng))
def check_inputs(d):
    b = []
    for k in ("x", "u", "v"):
        a = np.abs(d[k].astype(np.float32))
        if not (np.isfinite(a).all() and ((a == 0) | (a >= 2.0 ** -30) & (a <= 2.0 ** 30)).all()): b.append("a value of " + k)
    for k in ("l", "m"):
        if not ((d[k] >= 0) & (d[k] < C)).all(): b.append("an entry of " + k)
    none, least, most = [emit(mx_ref.quantize(np.full((128, 16), k, np.float32).astype(BF)))[1][0, 0] for k in (0.0, 2.0 ** -30, 2.0 ** 30)]
    for r in range(N):
        if ((d["wc"][r] == 0x7F) | (d["wc"][r] == 0xFF)).any(): b.append("wc: a code that is no number")
        s = mx_ref.live(d["ws"][r])
        if ((s != none) & ((s < least) | (s > most))).any(): b.append("ws: a scale out of range")
    return b
def reference(x, l, m, u, v, wc, ws):
    qu = [mx_ref.quantize(u[r]) for r in range(N)]
    lay = [pk(wc[r], ws[r]) for r in range(N)]
    first, second = [gentries(l[r]) for r in range(N)], [gentries(m[r]) for r in range(N)]
    now = [x[r] for r in range(N)]
    lanes = np.arange(8)[:, None]
    left, right = np.zeros((N, 8, K), np.int64), np.zeros((N, 8, K), np.int64)
    for t in range(R):
        own, packs = [], []
        for r in range(N):
            q = mx_ref.quantize(now[r])
            own.append(decode(q).astype(BF))
            s = mx_ref.matmul(qu[r], q) + np.float32(0.0)
            n = np.argsort(-s[::16], axis=1, kind="stable")[:, :K]
            a, b = first[r][lanes, n], second[r][lanes, n]
            word = np.stack([s[i::16] > 0 for i in range(1, 5)])
            wa, wb = word[:, lanes, a], word[:, lanes, b]
            straight = np.count_nonzero(wa == wa[:, :1], axis=0) + np.count_nonzero(wb == wb[:, :1], axis=0)
            crossed = np.count_nonzero(wb == wa[:, :1], axis=0) + np.count_nonzero(wa == wb[:, :1], axis=0)
            left[r] = np.where(crossed > straight, b, a)
            right[r] = np.where(crossed > straight, a, b)
            z = (gcols(own[r], left[r]).astype(np.float32) - gcols(own[r], right[r]).astype(np.float32)) * np.float32(0.5)
            packs.append(mx_ref.quantize(z.astype(BF)))
        for r in range(N):
            e = (r + 1 + t) % N
            h = mx_ref.quantize(tile([mx_ref.matmul(pick(lay[e], np.arange(128 * b, 128 * b + 128)), packs[r]) * np.float32(0.03125) for b in range(4)]))
            who = np.full((8, C), -1)
            for k in reversed(range(K)): who[np.arange(8), left[r][:, k]] = k
            now[r] = (own[r].astype(np.float32) + gcols(decode(h).astype(BF), who).astype(np.float32)).astype(BF)
    y, ol = np.zeros((N, 128, C), np.float32), np.zeros((N, 8, 2 * K), np.float32)
    oc, osc = np.zeros((N, 128, 4 * C), np.uint8), np.zeros((N, 16, C), np.uint8)
    for r in range(N):
        q = mx_ref.quantize(now[r])
        y[r] = mx_ref.matmul(mx_ref.quantize(v[r]), q)
        ol[r] = np.concatenate([left[r], right[r]], axis=1)
        oc[r], osc[r] = emit(q)
    return {"y": y, "ol": ol, "oc": oc, "osc": osc}

@@ -1,0 +1,456 @@
+from concourse.bass import DstId, RemoteDMATransfer
+from concourse.mybir import dt, AluOpType, ActivationFunctionType
+
+C, K, R = 288, 160, 3
+CB, KB = C // 16, K // 16
+BIG = 2.0 ** 96
+TINY = 2.0 ** -120
+LIFT, MID, LOW = 2.0 ** 20, 2.0 ** 16, 256.0
+ST = [0, 64, 128, 160, 160]
+SEG = [176 * c - 8 * c * c for c in range(KB + 1)]
+DW = 176
+Q8, U8, BF, F32, I32, U16 = "float8_e4m3fn_x4", "uint8", "bfloat16", "float32", "int32", "uint16"
+
+SCRATCH = {}
+
+
+def _sb(name, n, d):
+    SCRATCH[name] = ("sbuf", [128, n], d)
+
+
+for _n, _w in (("wq", 512), ("hq", 128), ("wl0", 512), ("wl1", 512), ("wl2", 512), ("xq", C), ("uq", 128), ("ub", 128),
+               ("vq", 128), ("eq", 512), ("gq", 384), ("zq", 160), ("dq", K), ("mq", K), ("rq", K),
+               ("cq0", C), ("cq1", C), ("cq2", C), ("cq3", C), ("cq4", C)):
+    _sb(_n, _w, Q8)
+    _sb(_n + "s", _w, U8)
+for _n, _w in (("xt", 4 * C), ("ut", 512), ("vt", 512), ("et", 2048), ("gt", 1536), ("ones", 512), ("zt", 640),
+               ("ident", 128), ("srow", C), ("m01", C), ("m1", C), ("r01", C), ("rst", C), ("sg", C), ("th", 4 * C),
+               ("tp", 2 * C), ("gd", 2 * C), ("junk", 2448), ("cd", C), ("dtile", 4 * K), ("rg", 4 * K), ("mt", 4 * K),
+               ("ht", 4 * K), ("dh", 4 * DW), ("rowf", K), ("ownb", 16), ("ee", 960), ("dr", 960), ("fl", 960),
+               ("who", C + K), ("whs", C), ("kbig", C), ("klow", C), ("kmid", K)):
+    _sb(_n, _w, BF)
+for _t in range(5):
+    _sb("ct%d" % _t, 4 * (C - ST[_t]), BF)
+for _n, _w in (("iota", C), ("lrow", C), ("lm", C), ("bm", C), ("lat", C), ("srt", C), ("pa", C), ("pb", C),
+               ("pw", C), ("qf", 8), ("col", 16), ("jw", 96), ("blk", 32), ("rows", 32), ("zz", 96),
+               ("lr", 32), ("oo", 96), ("r1", 2 * K), ("r2", 2 * K), ("yt", C), ("kcol", C)):
+    _sb(_n, _w, F32)
+for _n, _w in (("li", CB), ("mi", CB), ("pi", 16), ("abi", 32), ("fi", 32), ("ci", 16), ("gi", 32)):
+    _sb(_n, _w, I32)
+for _n, _w in (("lu", 32), ("mu", 32), ("pu", 16), ("qu", 32), ("gu", 32), ("ru", 32), ("abu", 32), ("lru", 32),
+               ("endu", 16), ("su", 16), ("wu", 32), ("revu", 32)):
+    _sb(_n, _w, U16)
+for _b in range(8):
+    SCRATCH["ps%d" % _b] = ("psum", [128, 512], F32)
+
+NDMA = 60
+SEMAPHORES = ["cv", "cs", "ct", "cg", "hin", "hout", "w0", "w1", "w2"] + ["d%d" % _i for _i in range(NDMA)]
+
+
+def _bits(engines):
+    m = 0
+    for e in engines:
+        m |= 1 << e
+    return m
+
+
+def _helpers(T, topo, r):
+    n = len(T.cores)
+    home = T.cores[r]
+    return [c for c in topo.cores_of(home)
+            if c != home and all(topo.may_write(c, T.cores[(r - 1 - t) % n]) for t in range(R))][:4]
+
+
+def _arrivals(T, topo, r, t):
+    e = (r + 1 + t) % len(T.cores)
+    return sum(2 * len(topo.engines(h, T.cores[r])) for h in _helpers(T, topo, e))
+
+
+def helper_program(g, core, T, topo, r, b):
+    n = len(T.cores)
+    share = len(topo.engines(T.cores[r], core)) // 4
+    g.wait_ge(T.sem.hin, 2 * share)
+    sent = 0
+    for t in range(R):
+        dst = T.cores[(r - 1 - t) % n]
+        rid, pid = topo.addr(dst, core)
+        mask = topo.mask(core, dst)
+        sem = T.sem["w%d" % t]
+        g.remote_dma(T["wl%d" % t][:, 128 * b:128 * b + 128].bitcast(dt.uint8), T.hq[:].bitcast(dt.uint8), sem,
+                     T.sem.hout, pid, rid, mask)
+        g.remote_dma(T["wl%ds" % t][:, 128 * b:128 * b + 128], T.hqs[:], sem, T.sem.hout, pid, rid, mask)
+        sent += 2 * len(topo.engines(core, dst))
+    g.wait_ge(T.sem.hout, sent)
+
+
+def rank_program(g, core, T, topo):
+    rank = T.rank_of(core)
+    if rank is None:
+        for r in range(len(T.cores)):
+            hs = _helpers(T, topo, r)
+            if core in hs:
+                helper_program(g, core, T, topo, r, hs.index(core))
+        return
+
+    A, F = AluOpType, ActivationFunctionType
+    V, S, PE, Y = g.vector, g.scalar, g.tensor, g.sync
+    queue = {"v": V, "s": S, "t": PE, "g": g, "y": Y}
+    count = {"v": 0, "s": 0, "t": 0, "g": 0}
+    waited = {q: {} for q in queue}
+    wrote, read = {}, {}
+    ndma = [0]
+
+    def need(q, tok):
+        sem, n = tok[0], tok[1]
+        if waited[q].get(sem, 0) < n:
+            queue[q].wait_ge(T.sem[sem], n)
+            waited[q][sem] = n
+
+    def order(q, r, w):
+        toks = []
+        for k in r:
+            toks += wrote.get(k, [])
+            if k.startswith("ps"):
+                toks += [x for x in read.get(k, []) if x[2] != q]
+        for k in w:
+            toks += wrote.get(k, []) + read.get(k, [])
+        if q == "t":
+            toks = [x for x in toks if x[2] != "t"]
+        best = {}
+        for x in toks:
+            best[x[0]] = max(best.get(x[0], 0), x[1])
+        for sem in best:
+            need(q, (sem, best[sem]))
+
+    def note(tok, r, w):
+        for k in r:
+            read.setdefault(k, []).append(tok)
+        for k in w:
+            wrote[k] = [tok]
+            read[k] = []
+
+    def op(q, fn, r, w):
+        order(q, r, w)
+        count[q] += 1
+        fn().then_inc(T.sem["c" + q], 1)
+        note(("c" + q, count[q], q), r, w)
+
+    def dma(q, out, in_, r, w):
+        order(q, r, w)
+        sem = "d%d" % ndma[0]
+        ndma[0] += 1
+        queue[q].dma_start(out, in_).then_inc(T.sem[sem], 16)
+        note((sem, 16, "dma"), r, w)
+
+    def ts(out, in0, s1, s2, o0, o1, r, w):
+        if o1 is None:
+            op("v", lambda: V.tensor_scalar(out, in0, s1, None, o0), r, w)
+        else:
+            op("v", lambda: V.tensor_scalar(out, in0, s1, s2, o0, o1), r, w)
+
+    def tt(out, a, b, o, r, w):
+        op("v", lambda: V.tensor_tensor(out, a, b, o), r, w)
+
+    def cp(out, in_, r, w):
+        op("v", lambda: V.tensor_copy(out, in_), r, w)
+
+    def scan(out, d0, d1, init, o0, o1, r, w):
+        op("v", lambda: V.tensor_tensor_scan(out, d0, d1, init, o0, o1), r, w)
+
+    def quant(name, a, b, tile, r, w=None):
+        op("v", lambda: V.quantize_mx(T[name][:, a:b], T[name + "s"][:, a:b], tile), r, [w or name])
+
+    def act(out, in_, func, r, w, **kw):
+        op("s", lambda: S.activation(out, in_, func, **kw), r, w)
+
+    def mm(bank, wname, w0, xname, n, start=True, stop=True, extra=(), x0=0):
+        op("t", lambda: PE.matmul_mx(T["ps%d" % bank][:, 0:n], T[wname][:, w0:w0 + 128], T[wname + "s"][:, w0:w0 + 128],
+                                     T[xname][:, x0:x0 + n], T[xname + "s"][:, x0:x0 + n], start, stop),
+           [wname, xname] + list(extra), ["ps%d" % bank])
+
+    def ps(bank, a, b):
+        return T["ps%d" % bank][:, a:b]
+
+    def weights():
+        for base, ws in ((0, (0.5, 8.0, 128.0, 2048.0)), (4, (2048.0, 128.0, 8.0, 0.5))):
+            act(T.col[:, base:base + 1], T.m01[:, 1:2], F.Copy, ["m01"], ["col%d" % base], scale=ws[0])
+        for i in range(1, 4):
+            for base, ws in ((0, (0.5, 8.0, 128.0, 2048.0)), (4, (2048.0, 128.0, 8.0, 0.5))):
+                act(T.col[:, base + i:base + i + 1], T.m01[:, 1 + i:2 + i], F.Identity, ["m01", "col%d" % (base + i - 1)],
+                    ["col%d" % (base + i)], scale=ws[i], bias=T.col[:, base + i - 1:base + i])
+        act(T.col[:, 8:9], T.col[:, 3:4], F.Copy, ["col3", "gb"], ["col8"], scale=T.blk[:, 16:17])
+        act(T.col[:, 10:11], T.col[:, 7:8], F.Copy, ["col7"], ["col10"], scale=-1.0)
+        act(T.col[:, 9:10], T.col[:, 8:9], F.Copy, ["col8"], ["col9"], scale=-1.0)
+
+    def tiles():
+        act(T.gt[:, 1024:1536], T.gt[:, 0:512], F.Copy, ["gt0", "col7"], ["gt2"], scale=T.col[:, 7:8])
+        act(T.gt[:, 512:1024], T.ones[:], F.Copy, ["ones", "col8"], ["gt1"], scale=T.col[:, 8:9])
+        act(T.gt[:, 1025:1536:4], T.gt[:, 0:512:4], F.Copy, ["gt0", "col10"], ["gt2"], scale=T.col[:, 10:11])
+        act(T.gt[:, 513:1024:4], T.ones[:, 0:128], F.Copy, ["ones", "col9"], ["gt1"], scale=T.col[:, 9:10])
+
+    def planes():
+        for b in range(4):
+            mm(2 + b, "eq", 128 * b, "xq", C)
+
+    def half(b):
+        act(T.th[:, C * b:C * b + C], ps(2 + b, 0, C), F.Copy, ["ps%d" % (2 + b)], ["th%d" % b], scale=0.5)
+
+    def whole():
+        act(T.tp[:], T.th[:, 0:2 * C], F.Copy, ["th0", "th1"], ["tp"], scale=2.0)
+
+    def nobody():
+        act(T.who[:, 0:C], T.srow[:], F.Identity, ["srow"], ["who"], scale=0.0, bias=float(K))
+
+    XT = ["xt0", "xt1", "xt2", "xt3"]
+    dma("y", T.xt[:], T.x[:], [], XT)
+    dma("s", T.ut[:], T.u[:], [], ["ut"])
+    dma("y", T.wq[:].bitcast(dt.uint8), T.wc[:], [], ["wq"])
+    dma("s", T.wqs[:], T.ws[:], [], ["wqs"])
+    dma("s", T.li[:], T.l[:], [], ["li"])
+    dma("s", T.mi[:], T.m[:], [], ["mi"])
+
+    q = T.qf[:, 0:1]
+    op("v", lambda: V.memset(T.zt[:], 0.0), [], ["zt"])
+    op("v", lambda: V.memset(T.ones[:], 1.0), [], ["ones"])
+    op("g", lambda: g.iota(T.ci[:, 0:1], [[0, 1]], 0, 1), [], ["ci0"])
+    op("g", lambda: g.iota(T.jw[:, 0:20], [[16, 20]], 0, 0, allow_small_or_imprecise_dtypes=True), [], ["jw"])
+    op("g", lambda: g.iota(T.gi[:], [[1, 8], [0, 4]], 0, 0), [], ["gi"])
+    op("g", lambda: g.iota(T.srow[:], [[0, CB], [1, 16]], 0, 0, allow_small_or_imprecise_dtypes=True), [], ["srow"])
+    op("g", lambda: g.affine_select(T.ident[:], T.ones[:, 0:128], [[-1, 128]], A.is_equal, 0.0, 0, 1), ["ones"], ["ident"])
+
+    for t in range(5):
+        n = (192, 192, 192, 320, 512)[t]
+        act(T["ct%d" % t][:, 0:n], T.zt[:, 0:n], F.Copy, ["zt"], ["c%d" % s for s in range(4 * t, 4 * t + 4)])
+    for b in range(4):
+        dma("y", T.et[:, 512 * b:512 * b + 512], T.zt[:, 0:512], ["zt"], ["et%d" % b])
+    quant("zq", 0, 160, T.zt[:], ["zt"])
+    for t in range(1, 5):
+        dma("y", T["cq%d" % t][:, 0:ST[t]].bitcast(dt.uint8), T.zq[:, 0:ST[t]].bitcast(dt.uint8), ["zq"], ["cqh%d" % t])
+        dma("y", T["cq%ds" % t][:, 0:ST[t]], T.zqs[:, 0:ST[t]], ["zq"], ["cqi%d" % t])
+    dma("y", T.dtile[:], T.zt[:], ["zt"], ["dt0", "dt1"])
+    dma("y", T.dr[:, 0:480], T.ones[:, 0:480], ["ones"], ["dra"])
+    dma("y", T.dr[:, 480:960], T.ones[:, 0:480], ["ones"], ["drb"])
+    dma("y", T.ee[:, 0:480], T.zt[:, 0:480], ["zt"], ["eea"])
+    dma("y", T.ee[:, 480:960], T.zt[:, 0:480], ["zt"], ["eeb"])
+    dma("y", T.vt[:], T.v[:], [], ["vt"])
+
+    op("v", lambda: V.memset(T.rows[:, CB - 1:CB], 0.0), [], ["rowz"])
+    op("v", lambda: V.memset(T.dh[:, K:4 * DW:DW], 0.0), [], ["dhz"])
+    ts(T.ci[:, 1:2], T.ci[:, 0:1], 15, None, A.bitwise_and, None, ["ci0"], ["ci1"])
+    cp(T.qf[:, 1:2], T.ci[:, 0:1], ["ci0"], ["p"])
+    cp(T.pu[:, 0:8], T.jw[:, 0:8], ["jw"], ["pu"])
+    cp(q, T.ci[:, 1:2], ["ci1"], ["q"])
+    cp(T.gu[:], T.gi[:], ["gi"], ["gu"])
+    ts(T.jw[:, 0:20], T.jw[:, 0:20], q, None, A.add, None, ["jw", "q"], ["jw"])
+    ts(T.qf[:, 2:3], q, 1.0, float(KB), A.add, A.min, ["q"], ["e0"])
+    ts(T.qu[:, 0:CB], T.zt[:, 0:CB], q, None, A.add, None, ["zt", "q"], ["qu"])
+    ts(T.blk[:, 16:24], T.jw[:, 0:8], T.qf[:, 1:2], None, A.is_equal, None, ["jw", "p"], ["gb"])
+    ts(T.qf[:, 3:4], T.qf[:, 2:3], -8.0, 176.0, A.mult, A.add, ["e0"], ["e1"])
+    ts(T.r01[:], T.srow[:], 0.0, None, A.not_equal, None, ["srow"], ["r01"])
+    ts(T.m01[:], T.srow[:], q, None, A.is_equal, None, ["srow", "q"], ["m01"])
+    ts(T.zz[:, 0:16], T.srow[:, 0:16], q, -1.0, A.is_lt, A.mult, ["srow", "q"], ["z1"])
+    ts(T.rst[:], T.r01[:], 2 * BIG, BIG, A.mult, A.subtract, ["r01"], ["rst"])
+    ts(T.m1[:], T.m01[:], 2 * BIG, BIG, A.mult, A.subtract, ["m01"], ["m1"])
+    tt(T.blk[:, 0:16], T.zz[:, 0:16], T.m01[:, 0:16], A.add, ["z1", "m01"], ["kb"])
+    ts(T.qf[:, 4:5], T.qf[:, 3:4], T.qf[:, 2:3], 1.0, A.mult, A.subtract, ["e0", "e1"], ["e2"])
+    ts(T.revu[:, 0:KB], T.jw[:, 0:KB], -1.0, float(K - 1), A.mult, A.add, ["jw"], ["rev0"])
+    ts(T.blk[:, 15:16], T.blk[:, 15:16], -2.0, None, A.add, None, ["kb"], ["kb"])
+    ts(T.revu[:, KB:2 * KB], T.jw[:, KB:2 * KB], -1.0, float(3 * K - 1), A.mult, A.add, ["jw"], ["rev1"])
+    cp(T.endu[:, 0:1], T.qf[:, 4:5], ["e2"], ["endu"])
+    act(T.gt[:, 0:512], T.blk[:, 16:24].indirect(T.gu[:]), F.Copy, ["gb", "gu"], ["gt0"])
+
+    quant("uq", 0, 128, T.ut[:], ["ut"])
+    cp(T.ub[:].bitcast(dt.uint32), T.uq[:].bitcast(dt.uint32).indirect(T.pu[:, 0:8]), ["uq", "pu"], ["ub"])
+    act(T.ubs[:], T.uqs[:].indirect(T.pu[:, 0:8]), F.Copy, ["uq", "pu"], ["ubs"])
+    weights()
+    act(T.kbig[:], T.blk[:, 0:16].indirect(T.qu[:, 0:CB]), F.Copy, ["kb", "qu"], ["kbig"], scale=LIFT)
+
+    hs = _helpers(T, topo, rank)
+    eng = topo.engines(core, hs[0])
+    share = len(eng) // 4
+    for name, land in (("wq", "hq"), ("wqs", "hqs")):
+        order("g", [name], [])
+        trs = []
+        for b, h in enumerate(hs):
+            rid, pid = topo.addr(h, core)
+            src, dst = T[name][:, 128 * b:128 * b + 128], T[land][:]
+            if name == "wq":
+                src, dst = src.bitcast(dt.uint8), dst.bitcast(dt.uint8)
+            trs.append(RemoteDMATransfer(dst_ids=[DstId(rid=rid, pnc=pid)],
+                                         dma_engine_mask=_bits(eng[share * b:share * b + share]),
+                                         remote_sem=T.sem.hin, src=src, dst=dst))
+        g.remote_dma_fused(trs, local_sem=T.sem.hout)
+    op("g", lambda: g.iota(T.iota[:], [[1, C]], 0, 0, allow_small_or_imprecise_dtypes=True), [], ["iota"])
+
+    for t in range(R):
+        last = t == R - 1
+        quant("xq", 0, C, T.xt[:], XT)
+        mm(0, "ub", 0, "xq", C, extra=["ubs"])
+        mm(1, "uq", 0, "xq", C)
+        if t == 0:
+            quant("gq", 0, 128, T.gt[:, 0:512], ["gt0"])
+            cp(T.lu[:, 0:CB], T.li[:], ["li"], ["lu"])
+            cp(T.mu[:, 0:CB], T.mi[:], ["mi"], ["mu"])
+        else:
+            planes()
+        if t == 1:
+            quant("vq", 0, 128, T.vt[:], ["vt"])
+        tt(T.bm[:], ps(0, 0, C), T.m1[:], A.min, ["ps0", "m1"], ["bm"])
+        scan(T.lat[:], T.rst[:], T.bm[:], -BIG, A.min, A.max, ["rst", "bm"], ["lat"])
+        act(T.sg[:], ps(1, 0, C), F.Sign, ["ps1"], ["sg"], bias=-TINY)
+        if t > 0:
+            half(0)
+        else:
+            act(T.kcol[:], T.kbig[:], F.Copy, ["kbig"], ["kcol"])
+            act(T.jw[:, 64:80], T.jw[:, 0:16], F.Identity, ["jw"], ["dump"], bias=float(C))
+        jo = 0
+        for s in (1, 0) + tuple(range(2, CB)):
+            tau, e = s // 4, s % 4
+            tile = T["ct%d" % tau]
+            if s == 0:
+                tt(tile[:, 0:4 * C:4], ps(0, 0, C), T.lat[:], A.is_le, ["ps0", "lat"], ["c0"])
+            else:
+                c = s - 1
+                a = 16 * c + 16
+                view = tile[:, 4 * (a - ST[tau]) + e:4 * (C - ST[tau]):4]
+                ts(view, ps(0, a, C), T.lat[:, 16 * c + 15:16 * c + 16], None, A.is_le, None, ["ps0", "lat"], ["c%d" % s])
+                act(T.junk[:, jo:jo + C - a], view, F.Copy, ["c%d" % s], ["junk%d" % c, "row%d" % c],
+                    accum_out=T.rows[:, c:c + 1])
+                jo += C - a
+            if t == 0 and 4 <= s < 8:
+                b = s - 4
+                act(T.et[:, 512 * b + b:512 * b + 512:4], T.ident[:], F.Copy, ["ident"], ["et%d" % b])
+            for tau in ([s // 4 - 1] if e == 0 and s else []) + ([4] if s == CB - 1 else []):
+                quant("cq%d" % tau, ST[tau], C, T["ct%d" % tau][:], ["c%d" % x for x in range(4 * tau, 4 * tau + 4)])
+                mm(6, "gq", 0, "cq%d" % tau, C, tau == 0, tau == 4, extra=["cqh%d" % tau, "cqi%d" % tau])
+                if t == 0 and tau == 2:
+                    tt(T.kcol[:, 15:C:16], T.kcol[:, 15:C:16], T.jw[:, 0:CB], A.subtract, ["kcol", "jw"], ["kcol"])
+                    act(T.lrow[:], T.iota[:].indirect(T.lu[:, 0:CB]), F.Copy, ["iota", "lu"], ["lrow"], scale=1024.0)
+        if t == 0:
+            quant("eq", 0, 512, T.et[:], ["et0", "et1", "et2", "et3"])
+            planes()
+        scan(T.cd[:], T.r01[:], T.ct0[:, 0:4 * C:4], 0.0, A.mult, A.add, ["r01", "c0"], ["cd"])
+        scan(T.pw[:], ps(6, 0, C), T.kcol[:], -LIFT, A.max, A.add, ["ps6", "kcol"], ["pw"])
+        tt(T.zz[:, 32:32 + CB], T.cd[:, 15:C:16], T.rows[:, 0:CB], A.add,
+           ["cd", "rowz"] + ["row%d" % c for c in range(CB - 1)], ["z2"])
+        if t == 0:
+            tt(T.lm[:], T.iota[:].indirect(T.mu[:, 0:CB]), T.lrow[:], A.add, ["iota", "mu", "lrow"], ["lm"])
+            tiles()
+            act(T.kmid[:], T.kbig[:, 0:K], F.Copy, ["kbig"], ["kmid"], scale=MID / LIFT)
+            half(0)
+        else:
+            for b in (1, 2, 3):
+                half(b)
+        tt(T.zz[:, 64:64 + CB], T.zz[:, 32:32 + CB], T.pw[:, 15:C:16], A.subtract, ["z2", "pw"], ["z3"])
+        ts(T.ru[:, 0:CB], T.zz[:, 64:64 + CB], -LIFT, None, A.add, None, ["z3"], ["ru"])
+        cp(T.srt[:].indirect(T.ru[:, 0:CB]), T.lm[:], ["ru", "lm"], ["srt"])
+        if t > 0:
+            whole()
+        scan(T.pa[:, 0:K], T.srt[:, C - K:C], T.kbig[:, 0:K], -LIFT, A.max, A.add, ["srt", "kbig"], ["pa"])
+        ts(T.pi[:, 0:KB], T.pa[:, 15:K:16], LIFT, None, A.add, None, ["pa"], ["pi"])
+        if t == 0:
+            quant("gq", 128, 384, T.gt[:, 512:1536], ["gt1", "gt2"], "gq2")
+        ts(T.abi[:, 0:KB], T.pi[:, 0:KB], 10, None, A.arith_shift_right, None, ["pi"], ["ai"])
+        ts(T.abi[:, KB:2 * KB], T.pi[:, 0:KB], 1023, None, A.bitwise_and, None, ["pi"], ["bi"])
+        cp(T.abu[:, 0:2 * KB], T.abi[:, 0:2 * KB], ["ai", "bi"], ["abu"])
+        cp(T.dtile[:, 0:4 * K:4], T.sg[:].indirect(T.abu[:, 0:KB]), ["sg", "abu"], ["dt0"])
+        act(T.dtile[:, 1:4 * K:4], T.sg[:].indirect(T.abu[:, KB:2 * KB]), F.Copy, ["sg", "abu"], ["dt1"])
+        if t == 0:
+            for b in (1, 2, 3):
+                half(b)
+            for c in range(KB):
+                act(T.dr[:, SEG[c] + 1:SEG[c] + 17], T.m01[:, 0:16], F.Identity, ["m01", "dra", "drb"], ["dr%d" % c],
+                    scale=-1.0, bias=1.0)
+        else:
+            nobody()
+        tt(T.oo[:, 32:32 + KB], T.abi[:, 0:KB], T.abi[:, KB:2 * KB], A.subtract, ["ai", "bi"], ["dd"])
+        quant("dq", 0, K, T.dtile[:], ["dt0", "dt1"])
+        mm(7, "gq", 128, "dq", K, extra=["gq2"])
+        mm(1, "gq", 256, "dq", K, extra=["gq2"])
+        scan(T.pa[:, 0:K], ps(7, 0, K), T.kmid[:], -MID, A.max, A.add, ["ps7", "kmid"], ["pa"])
+        scan(T.pb[:, 0:K], ps(1, 0, K), T.kmid[:], -MID, A.max, A.add, ["ps1", "kmid"], ["pb"])
+        tt(T.zz[:, 0:KB], T.pa[:, 15:K:16], T.pb[:, 15:K:16], A.mult, ["pa", "pb"], ["z1"])
+        ts(T.fi[:, 0:KB], T.zz[:, 0:KB], 2048.0 + 32768.0 - MID * MID, None, A.add, None, ["z1"], ["fi"])
+        ts(T.fi[:, 16:16 + KB], T.fi[:, 0:KB], 15, 1, A.arith_shift_right, A.bitwise_and, ["fi"], ["fj"])
+        tt(T.oo[:, 48:48 + KB], T.fi[:, 16:16 + KB], T.oo[:, 32:32 + KB], A.mult, ["fj", "dd"], ["ed"])
+        tt(T.lr[:, KB:2 * KB], T.abi[:, 0:KB], T.oo[:, 48:48 + KB], A.subtract, ["ai", "ed"], ["rf"])
+        tt(T.lr[:, 0:KB], T.abi[:, KB:2 * KB], T.oo[:, 48:48 + KB], A.add, ["bi", "ed"], ["lf"])
+        cp(T.lru[:, 0:2 * KB], T.lr[:, 0:2 * KB], ["lf", "rf"], ["lru"])
+        cp(T.rg[:, 0:K], T.th[:, 0:C].indirect(T.lru[:, KB:2 * KB]), ["th0", "lru"], ["rg0"])
+        for b in (1, 0, 2, 3):
+            win = T.th[:, C * b:C * b + C]
+            if b > 0:
+                act(T.rg[:, K * b:K * b + K], win.indirect(T.lru[:, KB:2 * KB]), F.Copy, ["th%d" % b, "lru"], ["rg%d" % b])
+            tt(T.mt[:, b:4 * K:4], win.indirect(T.lru[:, 0:KB]), T.rg[:, K * b:K * b + K], A.subtract,
+               ["th%d" % b, "lru", "rg%d" % b], ["mt%d" % b])
+        act(T.ownb[:, 0:KB], T.lr[:, 0:KB], F.Identity, ["lf"], ["ownb"], bias=-144.0)
+        act(T.rowf[:], T.iota[:].indirect(T.lru[:, 0:KB]), F.Identity, ["iota", "lru"], ["rowf"], bias=-144.0)
+        if t == 0:
+            nobody()
+
+        def repeats(c):
+            ts(T.ee[:, SEG[c]:SEG[c] + K - 16 * c], T.rowf[:, 16 * c:K], T.ownb[:, c:c + 1], None, A.is_equal, None,
+               ["rowf", "ownb", "eea", "eeb"], ["ee%d" % c])
+
+        repeats(KB - 1)
+        quant("mq", 0, K, T.mt[:], ["mt0", "mt1", "mt2", "mt3"])
+        need("t", ("w%d" % t, _arrivals(T, topo, rank, t)))
+        for b in range(4):
+            mm(2 + b, "wl%d" % t, 128 * b, "mq", K)
+            act(T.ht[:, b:4 * K:4], ps(2 + b, 0, K), F.Copy, ["ps%d" % (2 + b)], ["ht%d" % b], scale=0.03125)
+        for b in (2, 3):
+            mm(b, "eq", 128 * b, "xq", C)
+        if t == 0:
+            act(T.klow[:], T.kbig[:], F.Copy, ["kbig"], ["klow"], scale=LOW / LIFT)
+        for c in range(KB - 1):
+            repeats(c)
+        scan(T.fl[:], T.dr[:], T.ee[:], 0.0, A.mult, A.max,
+             ["ee%d" % c for c in range(KB)] + ["dr%d" % c for c in range(KB)], ["fl"])
+        quant("rq", 0, K, T.ht[:], ["ht0", "ht1", "ht2", "ht3"])
+        for b in range(4):
+            bank = (0, 1, 6, 7)[b]
+            mm(bank, "eq", 128 * b, "rq", K)
+            act(T.dh[:, DW * b:DW * b + K], ps(bank, 0, K), F.Copy, ["ps%d" % bank], ["dh%d" % b])
+            if t == 0 and b == 1:
+                whole()
+        tt(T.oo[:, 0:16], T.fl[:].indirect(T.endu[:, 0:1]), T.jw[:, 64:80], A.mult, ["fl", "endu", "dump"], ["o1"])
+        tt(T.oo[:, 16:16 + KB], T.oo[:, 0:KB], T.lr[:, 0:KB], A.max, ["o1", "lf"], ["o2"])
+        cp(T.su[:, 0:KB], T.oo[:, 16:16 + KB], ["o2"], ["su"])
+        cp(T.who[:].indirect(T.su[:, 0:KB]), T.iota[:, 0:K], ["su", "iota"], ["who"])
+        scan(T.whs[:], T.who[:, 0:C], T.klow[:], -LOW, A.max, A.add, ["who", "klow"], ["whs"])
+        ts(T.wu[:, 0:CB], T.whs[:, 15:C:16], LOW, None, A.add, None, ["whs"], ["wu"])
+        for b in (2, 3):
+            act(T.gd[:, C * (b - 2):C * (b - 1)], T.dh[:, DW * b:DW * b + K + 1].indirect(T.wu[:, 0:CB]), F.Copy,
+                ["dh%d" % b, "dhz", "wu"], ["gd%d" % b])
+        for b in (0, 1):
+            tt(T.xt[:, b:4 * C:4], T.dh[:, DW * b:DW * b + K + 1].indirect(T.wu[:, 0:CB]), T.tp[:, C * b:C * b + C], A.add,
+               ["dh%d" % b, "dhz", "wu", "tp"], ["xt%d" % b])
+        if last:
+            act(T.r1[:], T.iota[:].indirect(T.lru[:, 0:2 * KB]), F.Copy, ["iota", "lru"], ["r1"])
+            act(T.r2[:], T.r1[:].indirect(T.revu[:, 0:2 * KB]), F.Copy, ["r1", "rev0", "rev1"], ["r2"])
+            dma("y", T.ol[:], T.r2[0:128:16, :], ["r2"], [])
+        for b in (2, 3):
+            tt(T.xt[:, b:4 * C:4], ps(b, 0, C), T.gd[:, C * (b - 2):C * (b - 1)], A.add, ["ps%d" % b, "gd%d" % b],
+               ["xt%d" % b])
+
+    quant("xq", 0, C, T.xt[:], XT)
+    H = C // 2
+    mm(0, "vq", 0, "xq", H)
+    mm(1, "vq", 0, "xq", H, x0=H)
+    dma("y", T.oc[:], T.xq[:].bitcast(dt.uint8), ["xq"], [])
+    cp(T.yt[:, 0:H], ps(0, 0, H), ["ps0"], ["yt0"])
+    dma("s", T.osc[0:4, :], T.xqs[0:4, :], ["xq"], [])
+    act(T.yt[:, H:C], ps(1, 0, H), F.Copy, ["ps1"], ["yt1"])
+    dma("y", T.osc[4:8, :], T.xqs[32:36, :], ["xq"], [])
+    dma("y", T.y[:], T.yt[:], ["yt0", "yt1"], [])
+    for k in (2, 3):
+        dma("s", T.osc[4 * k:4 * k + 4, :], T.xqs[32 * k:32 * k + 4, :], ["xq"], [])
+
+    g.wait_ge(T.sem.hout, 8 * share)
+    need("g", ("cg", count["g"]))
+    need("t", ("ct", count["t"]))
+    need("v", ("cv", count["v"]))
+    need("s", ("cs", count["s"]))
+    for i in range(ndma[0]):
+        if not any(waited[x].get("d%d" % i, 0) for x in waited):
+            need("g", ("d%d" % i, 16))

@@ -5,10 +5,11 @@ C, K, R = 288, 160, 3
 CB, KB = C // 16, K // 16
 BIG = 2.0 ** 96
 TINY = 2.0 ** -120
-LIFT, MID, LOW = 2.0 ** 20, 2.0 ** 16, 256.0
+LIFT, MID, LOW = 2.0 ** 20, 2.0 ** 12, 256.0
 ST = [0, 64, 128, 160, 160]
 SEG = [176 * c - 8 * c * c for c in range(KB + 1)]
 DW = 176
+RISE = (1.0 / 32, 0.5, 8.0, 128.0)
 Q8, U8, BF, F32, I32, U16 = "float8_e4m3fn_x4", "uint8", "bfloat16", "float32", "int32", "uint16"
 
 SCRATCH = {}
@@ -25,20 +26,20 @@ for _n, _w in (("wq", 512), ("hq", 128), ("wl0", 512), ("wl1", 512), ("wl2", 512
     _sb(_n + "s", _w, U8)
 for _n, _w in (("xt", 4 * C), ("ut", 512), ("vt", 512), ("et", 2048), ("gt", 1536), ("ones", 512), ("zt", 640),
                ("ident", 128), ("srow", C), ("m01", C), ("m1", C), ("r01", C), ("rst", C), ("sg", C), ("th", 4 * C),
-               ("tp", 2 * C), ("gd", 2 * C), ("junk", 2448), ("cd", C), ("dtile", 4 * K), ("rg", 4 * K), ("mt", 4 * K),
-               ("ht", 4 * K), ("dh", 4 * DW), ("rowf", K), ("ownb", 16), ("ee", 960), ("dr", 960), ("fl", 960),
-               ("who", C + K), ("whs", C), ("kbig", C), ("klow", C), ("kmid", K)):
+               ("tp", 2 * C), ("gd", 2 * C), ("junk", 2448), ("cd", C), ("dtile", 4 * K), ("rg", 8 * K), ("mt", 4 * K),
+               ("ht", 4 * K), ("dh", 4 * DW), ("rowf", K), ("ownb", 32), ("ee", 960), ("dr", 960), ("fl", 960),
+               ("who", 960), ("whs", C), ("kbig", C), ("klow", C), ("kmid", K)):
     _sb(_n, _w, BF)
 for _t in range(5):
     _sb("ct%d" % _t, 4 * (C - ST[_t]), BF)
 for _n, _w in (("iota", C), ("lrow", C), ("lm", C), ("bm", C), ("lat", C), ("srt", C), ("pa", C), ("pb", C),
                ("pw", C), ("qf", 8), ("col", 16), ("jw", 96), ("blk", 32), ("rows", 32), ("zz", 96),
-               ("lr", 32), ("oo", 96), ("r1", 2 * K), ("r2", 2 * K), ("yt", C), ("kcol", C)):
+               ("lr", 32), ("oo", 96), ("r1", 2 * K), ("r2", 2 * K), ("yt", C), ("kcol", C), ("kq", K)):
     _sb(_n, _w, F32)
 for _n, _w in (("li", CB), ("mi", CB), ("pi", 16), ("abi", 32), ("fi", 32), ("ci", 16), ("gi", 32)):
     _sb(_n, _w, I32)
 for _n, _w in (("lu", 32), ("mu", 32), ("pu", 16), ("qu", 32), ("gu", 32), ("ru", 32), ("abu", 32), ("lru", 32),
-               ("endu", 16), ("su", 16), ("wu", 32), ("revu", 32)):
+               ("endu", 16), ("su", 32), ("wu", 32), ("revu", 32)):
     _sb(_n, _w, U16)
 for _b in range(8):
     SCRATCH["ps%d" % _b] = ("psum", [128, 512], F32)
@@ -172,10 +173,10 @@ def rank_program(g, core, T, topo):
         return T["ps%d" % bank][:, a:b]
 
     def weights():
-        for base, ws in ((0, (0.5, 8.0, 128.0, 2048.0)), (4, (2048.0, 128.0, 8.0, 0.5))):
+        for base, ws in ((0, RISE), (4, RISE[::-1])):
             act(T.col[:, base:base + 1], T.m01[:, 1:2], F.Copy, ["m01"], ["col%d" % base], scale=ws[0])
         for i in range(1, 4):
-            for base, ws in ((0, (0.5, 8.0, 128.0, 2048.0)), (4, (2048.0, 128.0, 8.0, 0.5))):
+            for base, ws in ((0, RISE), (4, RISE[::-1])):
                 act(T.col[:, base + i:base + i + 1], T.m01[:, 1 + i:2 + i], F.Identity, ["m01", "col%d" % (base + i - 1)],
                     ["col%d" % (base + i)], scale=ws[i], bias=T.col[:, base + i - 1:base + i])
         act(T.col[:, 8:9], T.col[:, 3:4], F.Copy, ["col3", "gb"], ["col8"], scale=T.blk[:, 16:17])
@@ -201,22 +202,35 @@ def rank_program(g, core, T, topo):
     def nobody():
         act(T.who[:, 0:C], T.srow[:], F.Identity, ["srow"], ["who"], scale=0.0, bias=float(K))
 
+    def diff(b):
+        tt(T.rg[:, K * (4 + b):K * (5 + b)], T.th[:, C * b:C * b + C].indirect(T.abu[:, 0:KB]), T.rg[:, K * b:K * b + K],
+           A.subtract, ["th%d" % b, "abu", "rg%d" % b], ["df%d" % b])
+
+    def pack(b):
+        tt(T.mt[:, b:4 * K:4], T.blk[:, 24:26].indirect(T.su[:, 16:16 + KB]), T.rg[:, K * (4 + b):K * (5 + b)], A.mult,
+           ["pm0", "pm1", "fu", "df%d" % b], ["mt%d" % b])
+
+    def repeats(c):
+        ts(T.ee[:, SEG[c]:SEG[c] + K - 16 * c], T.rowf[:, 16 * c:K], T.ownb[:, c:c + 1], T.ownb[:, 16 + c:17 + c],
+           A.is_equal, A.mult, ["rowf", "ownb", "dump", "eea", "eeb"], ["ee%d" % c])
+
     XT = ["xt0", "xt1", "xt2", "xt3"]
     dma("y", T.xt[:], T.x[:], [], XT)
     dma("s", T.ut[:], T.u[:], [], ["ut"])
     dma("y", T.wq[:].bitcast(dt.uint8), T.wc[:], [], ["wq"])
     dma("s", T.wqs[:], T.ws[:], [], ["wqs"])
-    dma("s", T.li[:], T.l[:], [], ["li"])
-    dma("s", T.mi[:], T.m[:], [], ["mi"])
+    dma("y", T.li[:], T.l[:], [], ["li"])
+    dma("y", T.mi[:], T.m[:], [], ["mi"])
 
     q = T.qf[:, 0:1]
     op("v", lambda: V.memset(T.zt[:], 0.0), [], ["zt"])
     op("v", lambda: V.memset(T.ones[:], 1.0), [], ["ones"])
     op("g", lambda: g.iota(T.ci[:, 0:1], [[0, 1]], 0, 1), [], ["ci0"])
     op("g", lambda: g.iota(T.jw[:, 0:20], [[16, 20]], 0, 0, allow_small_or_imprecise_dtypes=True), [], ["jw"])
-    op("g", lambda: g.iota(T.gi[:], [[1, 8], [0, 4]], 0, 0), [], ["gi"])
     op("g", lambda: g.iota(T.srow[:], [[0, CB], [1, 16]], 0, 0, allow_small_or_imprecise_dtypes=True), [], ["srow"])
+    op("g", lambda: g.iota(T.gi[:], [[1, 8], [0, 4]], 0, 0), [], ["gi"])
     op("g", lambda: g.affine_select(T.ident[:], T.ones[:, 0:128], [[-1, 128]], A.is_equal, 0.0, 0, 1), ["ones"], ["ident"])
+    op("g", lambda: g.iota(T.blk[:, 24:26], [[-2, 2]], 1, 0, allow_small_or_imprecise_dtypes=True), [], ["pm0", "pm1"])
 
     for t in range(5):
         n = (192, 192, 192, 320, 512)[t]
@@ -234,28 +248,26 @@ def rank_program(g, core, T, topo):
     dma("y", T.ee[:, 480:960], T.zt[:, 0:480], ["zt"], ["eeb"])
     dma("y", T.vt[:], T.v[:], [], ["vt"])
 
-    op("v", lambda: V.memset(T.rows[:, CB - 1:CB], 0.0), [], ["rowz"])
-    op("v", lambda: V.memset(T.dh[:, K:4 * DW:DW], 0.0), [], ["dhz"])
     ts(T.ci[:, 1:2], T.ci[:, 0:1], 15, None, A.bitwise_and, None, ["ci0"], ["ci1"])
     cp(T.qf[:, 1:2], T.ci[:, 0:1], ["ci0"], ["p"])
     cp(T.pu[:, 0:8], T.jw[:, 0:8], ["jw"], ["pu"])
     cp(q, T.ci[:, 1:2], ["ci1"], ["q"])
-    cp(T.gu[:], T.gi[:], ["gi"], ["gu"])
+    op("v", lambda: V.memset(T.rows[:, CB - 1:CB], 0.0), [], ["rowz"])
+    op("v", lambda: V.memset(T.dh[:, K:4 * DW:DW], 0.0), [], ["dhz"])
     ts(T.jw[:, 0:20], T.jw[:, 0:20], q, None, A.add, None, ["jw", "q"], ["jw"])
     ts(T.qf[:, 2:3], q, 1.0, float(KB), A.add, A.min, ["q"], ["e0"])
     ts(T.qu[:, 0:CB], T.zt[:, 0:CB], q, None, A.add, None, ["zt", "q"], ["qu"])
     ts(T.blk[:, 16:24], T.jw[:, 0:8], T.qf[:, 1:2], None, A.is_equal, None, ["jw", "p"], ["gb"])
     ts(T.qf[:, 3:4], T.qf[:, 2:3], -8.0, 176.0, A.mult, A.add, ["e0"], ["e1"])
-    ts(T.r01[:], T.srow[:], 0.0, None, A.not_equal, None, ["srow"], ["r01"])
     ts(T.m01[:], T.srow[:], q, None, A.is_equal, None, ["srow", "q"], ["m01"])
+    ts(T.r01[:], T.srow[:], 0.0, None, A.not_equal, None, ["srow"], ["r01"])
+    cp(T.gu[:], T.gi[:], ["gi"], ["gu"])
     ts(T.zz[:, 0:16], T.srow[:, 0:16], q, -1.0, A.is_lt, A.mult, ["srow", "q"], ["z1"])
     ts(T.rst[:], T.r01[:], 2 * BIG, BIG, A.mult, A.subtract, ["r01"], ["rst"])
     ts(T.m1[:], T.m01[:], 2 * BIG, BIG, A.mult, A.subtract, ["m01"], ["m1"])
     tt(T.blk[:, 0:16], T.zz[:, 0:16], T.m01[:, 0:16], A.add, ["z1", "m01"], ["kb"])
     ts(T.qf[:, 4:5], T.qf[:, 3:4], T.qf[:, 2:3], 1.0, A.mult, A.subtract, ["e0", "e1"], ["e2"])
-    ts(T.revu[:, 0:KB], T.jw[:, 0:KB], -1.0, float(K - 1), A.mult, A.add, ["jw"], ["rev0"])
     ts(T.blk[:, 15:16], T.blk[:, 15:16], -2.0, None, A.add, None, ["kb"], ["kb"])
-    ts(T.revu[:, KB:2 * KB], T.jw[:, KB:2 * KB], -1.0, float(3 * K - 1), A.mult, A.add, ["jw"], ["rev1"])
     cp(T.endu[:, 0:1], T.qf[:, 4:5], ["e2"], ["endu"])
     act(T.gt[:, 0:512], T.blk[:, 16:24].indirect(T.gu[:]), F.Copy, ["gb", "gu"], ["gt0"])
 
@@ -263,7 +275,6 @@ def rank_program(g, core, T, topo):
     cp(T.ub[:].bitcast(dt.uint32), T.uq[:].bitcast(dt.uint32).indirect(T.pu[:, 0:8]), ["uq", "pu"], ["ub"])
     act(T.ubs[:], T.uqs[:].indirect(T.pu[:, 0:8]), F.Copy, ["uq", "pu"], ["ubs"])
     weights()
-    act(T.kbig[:], T.blk[:, 0:16].indirect(T.qu[:, 0:CB]), F.Copy, ["kb", "qu"], ["kbig"], scale=LIFT)
 
     hs = _helpers(T, topo, rank)
     eng = topo.engines(core, hs[0])
@@ -295,14 +306,17 @@ def rank_program(g, core, T, topo):
             planes()
         if t == 1:
             quant("vq", 0, 128, T.vt[:], ["vt"])
+        if last:
+            ts(T.revu[:, 0:KB], T.jw[:, 0:KB], -1.0, float(K - 1), A.mult, A.add, ["jw"], ["rev0"])
+            ts(T.revu[:, KB:2 * KB], T.jw[:, KB:2 * KB], -1.0, float(3 * K - 1), A.mult, A.add, ["jw"], ["rev1"])
         tt(T.bm[:], ps(0, 0, C), T.m1[:], A.min, ["ps0", "m1"], ["bm"])
         scan(T.lat[:], T.rst[:], T.bm[:], -BIG, A.min, A.max, ["rst", "bm"], ["lat"])
-        act(T.sg[:], ps(1, 0, C), F.Sign, ["ps1"], ["sg"], bias=-TINY)
         if t > 0:
+            act(T.sg[:], ps(1, 0, C), F.Sign, ["ps1"], ["sg"], bias=-TINY)
             half(0)
         else:
+            act(T.kbig[:], T.blk[:, 0:16].indirect(T.qu[:, 0:CB]), F.Copy, ["kb", "qu"], ["kbig"], scale=LIFT)
             act(T.kcol[:], T.kbig[:], F.Copy, ["kbig"], ["kcol"])
-            act(T.jw[:, 64:80], T.jw[:, 0:16], F.Identity, ["jw"], ["dump"], bias=float(C))
         jo = 0
         for s in (1, 0) + tuple(range(2, CB)):
             tau, e = s // 4, s % 4
@@ -320,90 +334,107 @@ def rank_program(g, core, T, topo):
             if t == 0 and 4 <= s < 8:
                 b = s - 4
                 act(T.et[:, 512 * b + b:512 * b + 512:4], T.ident[:], F.Copy, ["ident"], ["et%d" % b])
+            if t == 0 and s == 9:
+                tt(T.jw[:, 32:32 + CB], T.kbig[:, 15:C:16], T.jw[:, 0:CB], A.subtract, ["kbig", "jw"], ["kc"])
+            if s == 14:
+                scan(T.cd[:], T.r01[:], T.ct0[:, 0:4 * C:4], 0.0, A.mult, A.add, ["r01", "c0"], ["cd"])
             for tau in ([s // 4 - 1] if e == 0 and s else []) + ([4] if s == CB - 1 else []):
+                if tau == 4:
+                    tt(T.zz[:, 32:32 + CB], T.jw[:, 32:32 + CB], T.cd[:, 15:C:16], A.subtract, ["cd", "kc"], ["z2"])
                 quant("cq%d" % tau, ST[tau], C, T["ct%d" % tau][:], ["c%d" % x for x in range(4 * tau, 4 * tau + 4)])
                 mm(6, "gq", 0, "cq%d" % tau, C, tau == 0, tau == 4, extra=["cqh%d" % tau, "cqi%d" % tau])
-                if t == 0 and tau == 2:
-                    tt(T.kcol[:, 15:C:16], T.kcol[:, 15:C:16], T.jw[:, 0:CB], A.subtract, ["kcol", "jw"], ["kcol"])
-                    act(T.lrow[:], T.iota[:].indirect(T.lu[:, 0:CB]), F.Copy, ["iota", "lu"], ["lrow"], scale=1024.0)
         if t == 0:
             quant("eq", 0, 512, T.et[:], ["et0", "et1", "et2", "et3"])
             planes()
-        scan(T.cd[:], T.r01[:], T.ct0[:, 0:4 * C:4], 0.0, A.mult, A.add, ["r01", "c0"], ["cd"])
+            act(T.lrow[:], T.iota[:].indirect(T.lu[:, 0:CB]), F.Copy, ["iota", "lu"], ["lrow"], scale=1024.0)
+        tt(T.kcol[:, 15:C:16], T.zz[:, 32:32 + CB], T.rows[:, 0:CB], A.subtract,
+           ["z2", "rowz"] + ["row%d" % c for c in range(CB - 1)], ["kcol"])
         scan(T.pw[:], ps(6, 0, C), T.kcol[:], -LIFT, A.max, A.add, ["ps6", "kcol"], ["pw"])
-        tt(T.zz[:, 32:32 + CB], T.cd[:, 15:C:16], T.rows[:, 0:CB], A.add,
-           ["cd", "rowz"] + ["row%d" % c for c in range(CB - 1)], ["z2"])
         if t == 0:
             tt(T.lm[:], T.iota[:].indirect(T.mu[:, 0:CB]), T.lrow[:], A.add, ["iota", "mu", "lrow"], ["lm"])
             tiles()
-            act(T.kmid[:], T.kbig[:, 0:K], F.Copy, ["kbig"], ["kmid"], scale=MID / LIFT)
+            act(T.sg[:], ps(1, 0, C), F.Sign, ["ps1"], ["sg"], bias=-TINY)
             half(0)
+            half(1)
         else:
             for b in (1, 2, 3):
                 half(b)
-        tt(T.zz[:, 64:64 + CB], T.zz[:, 32:32 + CB], T.pw[:, 15:C:16], A.subtract, ["z2", "pw"], ["z3"])
-        ts(T.ru[:, 0:CB], T.zz[:, 64:64 + CB], -LIFT, None, A.add, None, ["z3"], ["ru"])
+        ts(T.ru[:, 0:CB], T.pw[:, 15:C:16], -1.0, -LIFT, A.mult, A.add, ["pw"], ["ru"])
         cp(T.srt[:].indirect(T.ru[:, 0:CB]), T.lm[:], ["ru", "lm"], ["srt"])
         if t > 0:
             whole()
+            nobody()
         scan(T.pa[:, 0:K], T.srt[:, C - K:C], T.kbig[:, 0:K], -LIFT, A.max, A.add, ["srt", "kbig"], ["pa"])
+        if t == 0:
+            ts(T.kmid[:], T.kbig[:, 0:K], MID / LIFT, None, A.mult, None, ["kbig"], ["kmid"])
         ts(T.pi[:, 0:KB], T.pa[:, 15:K:16], LIFT, None, A.add, None, ["pa"], ["pi"])
         if t == 0:
-            quant("gq", 128, 384, T.gt[:, 512:1536], ["gt1", "gt2"], "gq2")
+            ts(T.kq[:], T.kbig[:, 0:K], MID / LIFT, None, A.mult, None, ["kbig"], ["kq"])
         ts(T.abi[:, 0:KB], T.pi[:, 0:KB], 10, None, A.arith_shift_right, None, ["pi"], ["ai"])
         ts(T.abi[:, KB:2 * KB], T.pi[:, 0:KB], 1023, None, A.bitwise_and, None, ["pi"], ["bi"])
+        if t == 0:
+            ts(T.kq[:, 15:K:16], T.kq[:, 15:K:16], -8.0 / MID, None, A.add, None, ["kq"], ["kq"])
         cp(T.abu[:, 0:2 * KB], T.abi[:, 0:2 * KB], ["ai", "bi"], ["abu"])
+        if t == 0:
+            quant("gq", 128, 384, T.gt[:, 512:1536], ["gt1", "gt2"], "gq2")
+        else:
+            tt(T.oo[:, 32:32 + KB], T.abi[:, 0:KB], T.abi[:, KB:2 * KB], A.subtract, ["ai", "bi"], ["dd"])
         cp(T.dtile[:, 0:4 * K:4], T.sg[:].indirect(T.abu[:, 0:KB]), ["sg", "abu"], ["dt0"])
         act(T.dtile[:, 1:4 * K:4], T.sg[:].indirect(T.abu[:, KB:2 * KB]), F.Copy, ["sg", "abu"], ["dt1"])
-        if t == 0:
-            for b in (1, 2, 3):
+        for b in range(4):
+            if t == 0 and b >= 2:
                 half(b)
-            for c in range(KB):
-                act(T.dr[:, SEG[c] + 1:SEG[c] + 17], T.m01[:, 0:16], F.Identity, ["m01", "dra", "drb"], ["dr%d" % c],
-                    scale=-1.0, bias=1.0)
-        else:
-            nobody()
-        tt(T.oo[:, 32:32 + KB], T.abi[:, 0:KB], T.abi[:, KB:2 * KB], A.subtract, ["ai", "bi"], ["dd"])
+            act(T.rg[:, K * b:K * b + K], T.th[:, C * b:C * b + C].indirect(T.abu[:, KB:2 * KB]), F.Copy,
+                ["th%d" % b, "abu"], ["rg%d" % b])
+        if t == 0:
+            tt(T.oo[:, 32:32 + KB], T.abi[:, 0:KB], T.abi[:, KB:2 * KB], A.subtract, ["ai", "bi"], ["dd"])
+            act(T.ownb[:, 16:32], T.jw[:, 0:16], F.Identity, ["jw"], ["dump"], scale=4.0, bias=320.0)
         quant("dq", 0, K, T.dtile[:], ["dt0", "dt1"])
         mm(7, "gq", 128, "dq", K, extra=["gq2"])
         mm(1, "gq", 256, "dq", K, extra=["gq2"])
+        diff(0)
         scan(T.pa[:, 0:K], ps(7, 0, K), T.kmid[:], -MID, A.max, A.add, ["ps7", "kmid"], ["pa"])
-        scan(T.pb[:, 0:K], ps(1, 0, K), T.kmid[:], -MID, A.max, A.add, ["ps1", "kmid"], ["pb"])
-        tt(T.zz[:, 0:KB], T.pa[:, 15:K:16], T.pb[:, 15:K:16], A.mult, ["pa", "pb"], ["z1"])
-        ts(T.fi[:, 0:KB], T.zz[:, 0:KB], 2048.0 + 32768.0 - MID * MID, None, A.add, None, ["z1"], ["fi"])
-        ts(T.fi[:, 16:16 + KB], T.fi[:, 0:KB], 15, 1, A.arith_shift_right, A.bitwise_and, ["fi"], ["fj"])
+        scan(T.pb[:, 0:K], ps(1, 0, K), T.kq[:], -MID, A.max, A.add, ["ps1", "kq"], ["pb"])
+        diff(1)
+        tt(T.fi[:, 0:KB], T.pa[:, 15:K:16], T.pb[:, 15:K:16], A.mult, ["pa", "pb"], ["fi"])
+        diff(2)
+        ts(T.fi[:, 16:16 + KB], T.fi[:, 0:KB], 7, 1, A.arith_shift_right, A.bitwise_and, ["fi"], ["fj"])
+        diff(3)
+        cp(T.su[:, 16:16 + KB], T.fi[:, 16:16 + KB], ["fj"], ["fu"])
         tt(T.oo[:, 48:48 + KB], T.fi[:, 16:16 + KB], T.oo[:, 32:32 + KB], A.mult, ["fj", "dd"], ["ed"])
-        tt(T.lr[:, KB:2 * KB], T.abi[:, 0:KB], T.oo[:, 48:48 + KB], A.subtract, ["ai", "ed"], ["rf"])
-        tt(T.lr[:, 0:KB], T.abi[:, KB:2 * KB], T.oo[:, 48:48 + KB], A.add, ["bi", "ed"], ["lf"])
+        pack(0)
+        tt(T.lr[:, 0:KB], T.abi[:, 0:KB], T.oo[:, 48:48 + KB], A.subtract, ["ai", "ed"], ["lf"])
+        tt(T.lr[:, KB:2 * KB], T.abi[:, KB:2 * KB], T.oo[:, 48:48 + KB], A.add, ["bi", "ed"], ["rf"])
+        pack(1)
         cp(T.lru[:, 0:2 * KB], T.lr[:, 0:2 * KB], ["lf", "rf"], ["lru"])
-        cp(T.rg[:, 0:K], T.th[:, 0:C].indirect(T.lru[:, KB:2 * KB]), ["th0", "lru"], ["rg0"])
-        for b in (1, 0, 2, 3):
-            win = T.th[:, C * b:C * b + C]
-            if b > 0:
-                act(T.rg[:, K * b:K * b + K], win.indirect(T.lru[:, KB:2 * KB]), F.Copy, ["th%d" % b, "lru"], ["rg%d" % b])
-            tt(T.mt[:, b:4 * K:4], win.indirect(T.lru[:, 0:KB]), T.rg[:, K * b:K * b + K], A.subtract,
-               ["th%d" % b, "lru", "rg%d" % b], ["mt%d" % b])
         act(T.ownb[:, 0:KB], T.lr[:, 0:KB], F.Identity, ["lf"], ["ownb"], bias=-144.0)
         act(T.rowf[:], T.iota[:].indirect(T.lru[:, 0:KB]), F.Identity, ["iota", "lru"], ["rowf"], bias=-144.0)
+        pack(2)
+        pack(3)
         if t == 0:
-            nobody()
-
-        def repeats(c):
-            ts(T.ee[:, SEG[c]:SEG[c] + K - 16 * c], T.rowf[:, 16 * c:K], T.ownb[:, c:c + 1], None, A.is_equal, None,
-               ["rowf", "ownb", "eea", "eeb"], ["ee%d" % c])
-
-        repeats(KB - 1)
-        quant("mq", 0, K, T.mt[:], ["mt0", "mt1", "mt2", "mt3"])
+            for c in range(KB):
+                if c < 4:
+                    act(T.dr[:, SEG[c] + 1:SEG[c] + 17], T.m01[:, 0:16], F.Identity, ["m01", "dra", "drb"], ["dr%d" % c],
+                        scale=-1.0, bias=1.0)
+                else:
+                    ts(T.dr[:, SEG[c] + 1:SEG[c] + 17], T.m01[:, 0:16], -1.0, 1.0, A.mult, A.add, ["m01", "dra", "drb"],
+                       ["dr%d" % c])
+                if c == 5:
+                    quant("mq", 0, K, T.mt[:], ["mt0", "mt1", "mt2", "mt3"])
+        else:
+            repeats(KB - 1)
+            quant("mq", 0, K, T.mt[:], ["mt0", "mt1", "mt2", "mt3"])
         need("t", ("w%d" % t, _arrivals(T, topo, rank, t)))
         for b in range(4):
             mm(2 + b, "wl%d" % t, 128 * b, "mq", K)
             act(T.ht[:, b:4 * K:4], ps(2 + b, 0, K), F.Copy, ["ps%d" % (2 + b)], ["ht%d" % b], scale=0.03125)
         for b in (2, 3):
             mm(b, "eq", 128 * b, "xq", C)
-        if t == 0:
-            act(T.klow[:], T.kbig[:], F.Copy, ["kbig"], ["klow"], scale=LOW / LIFT)
-        for c in range(KB - 1):
+        for c in range(KB if t == 0 else KB - 1):
             repeats(c)
+        if t == 0:
+            nobody()
+            act(T.klow[:], T.kbig[:], F.Copy, ["kbig"], ["klow"], scale=LOW / LIFT)
         scan(T.fl[:], T.dr[:], T.ee[:], 0.0, A.mult, A.max,
              ["ee%d" % c for c in range(KB)] + ["dr%d" % c for c in range(KB)], ["fl"])
         quant("rq", 0, K, T.ht[:], ["ht0", "ht1", "ht2", "ht3"])
@@ -413,9 +444,8 @@ def rank_program(g, core, T, topo):
             act(T.dh[:, DW * b:DW * b + K], ps(bank, 0, K), F.Copy, ["ps%d" % bank], ["dh%d" % b])
             if t == 0 and b == 1:
                 whole()
-        tt(T.oo[:, 0:16], T.fl[:].indirect(T.endu[:, 0:1]), T.jw[:, 64:80], A.mult, ["fl", "endu", "dump"], ["o1"])
-        tt(T.oo[:, 16:16 + KB], T.oo[:, 0:KB], T.lr[:, 0:KB], A.max, ["o1", "lf"], ["o2"])
-        cp(T.su[:, 0:KB], T.oo[:, 16:16 + KB], ["o2"], ["su"])
+        tt(T.oo[:, 0:16], T.fl[:].indirect(T.endu[:, 0:1]), T.lr[:, 0:16], A.max, ["fl", "endu", "lf", "rf"], ["o1"])
+        cp(T.su[:, 0:KB], T.oo[:, 0:KB], ["o1"], ["su"])
         cp(T.who[:].indirect(T.su[:, 0:KB]), T.iota[:, 0:K], ["su", "iota"], ["who"])
         scan(T.whs[:], T.who[:, 0:C], T.klow[:], -LOW, A.max, A.add, ["who", "klow"], ["whs"])
         ts(T.wu[:, 0:CB], T.whs[:, 15:C:16], LOW, None, A.add, None, ["whs"], ["wu"])

@@ -3,6 +3,7 @@ from concourse.mybir import dt, AluOpType, ActivationFunctionType
 
 C, K, R = 288, 160, 3
 CB, KB = C // 16, K // 16
+H = C // 2
 BIG = 2.0 ** 96
 TINY = 2.0 ** -120
 LIFT, MID, LOW = 2.0 ** 20, 2.0 ** 12, 256.0
@@ -25,7 +26,7 @@ for _n, _w in (("wq", 512), ("hq", 128), ("wl0", 512), ("wl1", 512), ("wl2", 512
     _sb(_n, _w, Q8)
     _sb(_n + "s", _w, U8)
 for _n, _w in (("xt", 4 * C), ("ut", 512), ("vt", 512), ("et", 2048), ("gt", 1536), ("ones", 512), ("zt", 640),
-               ("ident", 128), ("srow", C), ("m01", C), ("m1", C), ("r01", C), ("rst", C), ("sg", C), ("th", 4 * C),
+               ("srow", C), ("m01", C), ("m1", C), ("r01", C), ("rst", C), ("sg", C), ("th", 4 * C),
                ("tp", 2 * C), ("gd", 2 * C), ("junk", 2448), ("cd", C), ("dtile", 4 * K), ("rg", 8 * K), ("mt", 4 * K),
                ("ht", 4 * K), ("dh", 4 * DW), ("rowf", K), ("ownb", 32), ("ee", 960), ("dr", 960), ("fl", 960),
                ("who", 960), ("whs", C), ("kbig", C), ("klow", C), ("kmid", K)):
@@ -214,6 +215,14 @@ def rank_program(g, core, T, topo):
         ts(T.ee[:, SEG[c]:SEG[c] + K - 16 * c], T.rowf[:, 16 * c:K], T.ownb[:, c:c + 1], T.ownb[:, 16 + c:17 + c],
            A.is_equal, A.mult, ["rowf", "ownb", "dump", "eea", "eeb"], ["ee%d" % c])
 
+    def repeated(c0, c1):
+        scan(T.fl[:, SEG[c0]:SEG[c1]], T.dr[:, SEG[c0]:SEG[c1]], T.ee[:, SEG[c0]:SEG[c1]], 0.0, A.mult, A.max,
+             ["ee%d" % c for c in range(c0, c1)] + ["dr%d" % c for c in range(c0, c1)], ["fl%d" % c0])
+
+    def sums(tau):
+        quant("cq%d" % tau, ST[tau], C, T["ct%d" % tau][:], ["c%d" % x for x in range(4 * tau, 4 * tau + 4)])
+        mm(6, "gq", 0, "cq%d" % tau, C, tau == 0, tau == 4, extra=["cqh%d" % tau, "cqi%d" % tau])
+
     XT = ["xt0", "xt1", "xt2", "xt3"]
     dma("y", T.xt[:], T.x[:], [], XT)
     dma("s", T.ut[:], T.u[:], [], ["ut"])
@@ -229,8 +238,8 @@ def rank_program(g, core, T, topo):
     op("g", lambda: g.iota(T.jw[:, 0:20], [[16, 20]], 0, 0, allow_small_or_imprecise_dtypes=True), [], ["jw"])
     op("g", lambda: g.iota(T.srow[:], [[0, CB], [1, 16]], 0, 0, allow_small_or_imprecise_dtypes=True), [], ["srow"])
     op("g", lambda: g.iota(T.gi[:], [[1, 8], [0, 4]], 0, 0), [], ["gi"])
-    op("g", lambda: g.affine_select(T.ident[:], T.ones[:, 0:128], [[-1, 128]], A.is_equal, 0.0, 0, 1), ["ones"], ["ident"])
     op("g", lambda: g.iota(T.blk[:, 24:26], [[-2, 2]], 1, 0, allow_small_or_imprecise_dtypes=True), [], ["pm0", "pm1"])
+    op("g", lambda: g.iota(T.iota[:], [[1, C]], 0, 0, allow_small_or_imprecise_dtypes=True), [], ["iota"])
 
     for t in range(5):
         n = (192, 192, 192, 320, 512)[t]
@@ -251,27 +260,27 @@ def rank_program(g, core, T, topo):
     ts(T.ci[:, 1:2], T.ci[:, 0:1], 15, None, A.bitwise_and, None, ["ci0"], ["ci1"])
     cp(T.qf[:, 1:2], T.ci[:, 0:1], ["ci0"], ["p"])
     cp(T.pu[:, 0:8], T.jw[:, 0:8], ["jw"], ["pu"])
-    cp(q, T.ci[:, 1:2], ["ci1"], ["q"])
     op("v", lambda: V.memset(T.rows[:, CB - 1:CB], 0.0), [], ["rowz"])
+    cp(q, T.ci[:, 1:2], ["ci1"], ["q"])
     op("v", lambda: V.memset(T.dh[:, K:4 * DW:DW], 0.0), [], ["dhz"])
-    ts(T.jw[:, 0:20], T.jw[:, 0:20], q, None, A.add, None, ["jw", "q"], ["jw"])
-    ts(T.qf[:, 2:3], q, 1.0, float(KB), A.add, A.min, ["q"], ["e0"])
-    ts(T.qu[:, 0:CB], T.zt[:, 0:CB], q, None, A.add, None, ["zt", "q"], ["qu"])
-    ts(T.blk[:, 16:24], T.jw[:, 0:8], T.qf[:, 1:2], None, A.is_equal, None, ["jw", "p"], ["gb"])
-    ts(T.qf[:, 3:4], T.qf[:, 2:3], -8.0, 176.0, A.mult, A.add, ["e0"], ["e1"])
-    ts(T.m01[:], T.srow[:], q, None, A.is_equal, None, ["srow", "q"], ["m01"])
     ts(T.r01[:], T.srow[:], 0.0, None, A.not_equal, None, ["srow"], ["r01"])
+    ts(T.jw[:, 0:20], T.jw[:, 0:20], q, None, A.add, None, ["jw", "q"], ["jw"])
+    ts(T.m01[:], T.srow[:], q, None, A.is_equal, None, ["srow", "q"], ["m01"])
+    ts(T.qf[:, 2:3], q, 1.0, float(KB), A.add, A.min, ["q"], ["e0"])
     cp(T.gu[:], T.gi[:], ["gi"], ["gu"])
+    ts(T.blk[:, 16:24], T.jw[:, 0:8], T.qf[:, 1:2], None, A.is_equal, None, ["jw", "p"], ["gb"])
     ts(T.zz[:, 0:16], T.srow[:, 0:16], q, -1.0, A.is_lt, A.mult, ["srow", "q"], ["z1"])
+    ts(T.qu[:, 0:CB], T.zt[:, 0:CB], q, None, A.add, None, ["zt", "q"], ["qu"])
+    ts(T.qf[:, 3:4], T.qf[:, 2:3], -8.0, 176.0, A.mult, A.add, ["e0"], ["e1"])
     ts(T.rst[:], T.r01[:], 2 * BIG, BIG, A.mult, A.subtract, ["r01"], ["rst"])
-    ts(T.m1[:], T.m01[:], 2 * BIG, BIG, A.mult, A.subtract, ["m01"], ["m1"])
     tt(T.blk[:, 0:16], T.zz[:, 0:16], T.m01[:, 0:16], A.add, ["z1", "m01"], ["kb"])
+    ts(T.m1[:], T.m01[:], 2 * BIG, BIG, A.mult, A.subtract, ["m01"], ["m1"])
     ts(T.qf[:, 4:5], T.qf[:, 3:4], T.qf[:, 2:3], 1.0, A.mult, A.subtract, ["e0", "e1"], ["e2"])
     ts(T.blk[:, 15:16], T.blk[:, 15:16], -2.0, None, A.add, None, ["kb"], ["kb"])
-    cp(T.endu[:, 0:1], T.qf[:, 4:5], ["e2"], ["endu"])
     act(T.gt[:, 0:512], T.blk[:, 16:24].indirect(T.gu[:]), F.Copy, ["gb", "gu"], ["gt0"])
 
     quant("uq", 0, 128, T.ut[:], ["ut"])
+    cp(T.endu[:, 0:1], T.qf[:, 4:5], ["e2"], ["endu"])
     cp(T.ub[:].bitcast(dt.uint32), T.uq[:].bitcast(dt.uint32).indirect(T.pu[:, 0:8]), ["uq", "pu"], ["ub"])
     act(T.ubs[:], T.uqs[:].indirect(T.pu[:, 0:8]), F.Copy, ["uq", "pu"], ["ubs"])
     weights()
@@ -291,7 +300,9 @@ def rank_program(g, core, T, topo):
                                          dma_engine_mask=_bits(eng[share * b:share * b + share]),
                                          remote_sem=T.sem.hin, src=src, dst=dst))
         g.remote_dma_fused(trs, local_sem=T.sem.hout)
-    op("g", lambda: g.iota(T.iota[:], [[1, C]], 0, 0, allow_small_or_imprecise_dtypes=True), [], ["iota"])
+    for b in range(4):
+        op("g", lambda: g.affine_select(T.et[:, 512 * b + b:512 * b + 512:4], T.ones[:, 0:128], [[-1, 128]], A.is_equal,
+                                        0.0, 0, 1), ["ones"], ["et%d" % b])
 
     for t in range(R):
         last = t == R - 1
@@ -309,71 +320,81 @@ def rank_program(g, core, T, topo):
         if last:
             ts(T.revu[:, 0:KB], T.jw[:, 0:KB], -1.0, float(K - 1), A.mult, A.add, ["jw"], ["rev0"])
             ts(T.revu[:, KB:2 * KB], T.jw[:, KB:2 * KB], -1.0, float(3 * K - 1), A.mult, A.add, ["jw"], ["rev1"])
-        tt(T.bm[:], ps(0, 0, C), T.m1[:], A.min, ["ps0", "m1"], ["bm"])
-        scan(T.lat[:], T.rst[:], T.bm[:], -BIG, A.min, A.max, ["rst", "bm"], ["lat"])
+        for h in range(2):
+            tt(T.bm[:, H * h:H * h + H], ps(0, H * h, H * h + H), T.m1[:, 0:H], A.min, ["ps0", "m1"], ["bm%d" % h])
+        for h in range(2):
+            scan(T.lat[:, H * h:H * h + H], T.rst[:, 0:H], T.bm[:, H * h:H * h + H], -BIG, A.min, A.max,
+                 ["rst", "bm%d" % h], ["lat%d" % h])
         if t > 0:
             act(T.sg[:], ps(1, 0, C), F.Sign, ["ps1"], ["sg"], bias=-TINY)
             half(0)
         else:
             act(T.kbig[:], T.blk[:, 0:16].indirect(T.qu[:, 0:CB]), F.Copy, ["kb", "qu"], ["kbig"], scale=LIFT)
-            act(T.kcol[:], T.kbig[:], F.Copy, ["kbig"], ["kcol"])
         jo = 0
         for s in (1, 0) + tuple(range(2, CB)):
             tau, e = s // 4, s % 4
             tile = T["ct%d" % tau]
             if s == 0:
-                tt(tile[:, 0:4 * C:4], ps(0, 0, C), T.lat[:], A.is_le, ["ps0", "lat"], ["c0"])
+                tt(tile[:, 0:4 * C:4], ps(0, 0, C), T.lat[:], A.is_le, ["ps0", "lat0", "lat1"], ["c0"])
             else:
                 c = s - 1
                 a = 16 * c + 16
                 view = tile[:, 4 * (a - ST[tau]) + e:4 * (C - ST[tau]):4]
-                ts(view, ps(0, a, C), T.lat[:, 16 * c + 15:16 * c + 16], None, A.is_le, None, ["ps0", "lat"], ["c%d" % s])
+                ts(view, ps(0, a, C), T.lat[:, 16 * c + 15:16 * c + 16], None, A.is_le, None,
+                   ["ps0", "lat%d" % (16 * c // H)], ["c%d" % s])
                 act(T.junk[:, jo:jo + C - a], view, F.Copy, ["c%d" % s], ["junk%d" % c, "row%d" % c],
                     accum_out=T.rows[:, c:c + 1])
                 jo += C - a
-            if t == 0 and 4 <= s < 8:
-                b = s - 4
-                act(T.et[:, 512 * b + b:512 * b + 512:4], T.ident[:], F.Copy, ["ident"], ["et%d" % b])
+            if t == 0 and s == 1:
+                act(T.kcol[:], T.kbig[:], F.Copy, ["kbig"], ["kcol"])
             if t == 0 and s == 9:
                 tt(T.jw[:, 32:32 + CB], T.kbig[:, 15:C:16], T.jw[:, 0:CB], A.subtract, ["kbig", "jw"], ["kc"])
-            if s == 14:
-                scan(T.cd[:], T.r01[:], T.ct0[:, 0:4 * C:4], 0.0, A.mult, A.add, ["r01", "c0"], ["cd"])
-            for tau in ([s // 4 - 1] if e == 0 and s else []) + ([4] if s == CB - 1 else []):
-                if tau == 4:
-                    tt(T.zz[:, 32:32 + CB], T.jw[:, 32:32 + CB], T.cd[:, 15:C:16], A.subtract, ["cd", "kc"], ["z2"])
-                quant("cq%d" % tau, ST[tau], C, T["ct%d" % tau][:], ["c%d" % x for x in range(4 * tau, 4 * tau + 4)])
-                mm(6, "gq", 0, "cq%d" % tau, C, tau == 0, tau == 4, extra=["cqh%d" % tau, "cqi%d" % tau])
+            if s in (4, 9, 14, 17):
+                sums((4, 9, 14, 17).index(s))
+        scan(T.cd[:], T.r01[:], T.ct0[:, 0:4 * C:4], 0.0, A.mult, A.add, ["r01", "c0"], ["cd"])
+        sums(4)
+        if t == 0:
+            act(T.lrow[:], T.iota[:].indirect(T.lu[:, 0:CB]), F.Copy, ["iota", "lu"], ["lrow"], scale=1024.0)
+        tt(T.zz[:, 32:32 + CB], T.jw[:, 32:32 + CB], T.cd[:, 15:C:16], A.subtract, ["cd", "kc"], ["z2"])
         if t == 0:
             quant("eq", 0, 512, T.et[:], ["et0", "et1", "et2", "et3"])
             planes()
-            act(T.lrow[:], T.iota[:].indirect(T.lu[:, 0:CB]), F.Copy, ["iota", "lu"], ["lrow"], scale=1024.0)
         tt(T.kcol[:, 15:C:16], T.zz[:, 32:32 + CB], T.rows[:, 0:CB], A.subtract,
            ["z2", "rowz"] + ["row%d" % c for c in range(CB - 1)], ["kcol"])
+        if t == 0:
+            ts(T.kmid[:], T.kbig[:, 0:K], MID / LIFT, None, A.mult, None, ["kbig"], ["kmid"])
+            ts(T.kq[:], T.kbig[:, 0:K], MID / LIFT, None, A.mult, None, ["kbig"], ["kq"])
         scan(T.pw[:], ps(6, 0, C), T.kcol[:], -LIFT, A.max, A.add, ["ps6", "kcol"], ["pw"])
         if t == 0:
             tt(T.lm[:], T.iota[:].indirect(T.mu[:, 0:CB]), T.lrow[:], A.add, ["iota", "mu", "lrow"], ["lm"])
             tiles()
             act(T.sg[:], ps(1, 0, C), F.Sign, ["ps1"], ["sg"], bias=-TINY)
             half(0)
-            half(1)
-        else:
-            for b in (1, 2, 3):
-                half(b)
+        for b in (1, 2, 3):
+            half(b)
         ts(T.ru[:, 0:CB], T.pw[:, 15:C:16], -1.0, -LIFT, A.mult, A.add, ["pw"], ["ru"])
+        if t == 0:
+            ts(T.klow[:], T.kbig[:], LOW / LIFT, None, A.mult, None, ["kbig"], ["klow"])
         cp(T.srt[:].indirect(T.ru[:, 0:CB]), T.lm[:], ["ru", "lm"], ["srt"])
         if t > 0:
             whole()
             nobody()
+        else:
+            ts(T.kq[:, 15:K:16], T.kq[:, 15:K:16], -8.0 / MID, None, A.add, None, ["kq"], ["kq"])
+
+        def resets(cs):
+            for c in cs if t == 0 else ():
+                ts(T.dr[:, SEG[c] + 1:SEG[c] + 17], T.m01[:, 0:16], -1.0, 1.0, A.mult, A.add, ["m01", "dra", "drb"],
+                   ["dr%d" % c])
+
+        resets((9,))
         scan(T.pa[:, 0:K], T.srt[:, C - K:C], T.kbig[:, 0:K], -LIFT, A.max, A.add, ["srt", "kbig"], ["pa"])
-        if t == 0:
-            ts(T.kmid[:], T.kbig[:, 0:K], MID / LIFT, None, A.mult, None, ["kbig"], ["kmid"])
+        resets((0, 1, 2))
         ts(T.pi[:, 0:KB], T.pa[:, 15:K:16], LIFT, None, A.add, None, ["pa"], ["pi"])
-        if t == 0:
-            ts(T.kq[:], T.kbig[:, 0:K], MID / LIFT, None, A.mult, None, ["kbig"], ["kq"])
+        resets((3, 4, 5))
         ts(T.abi[:, 0:KB], T.pi[:, 0:KB], 10, None, A.arith_shift_right, None, ["pi"], ["ai"])
         ts(T.abi[:, KB:2 * KB], T.pi[:, 0:KB], 1023, None, A.bitwise_and, None, ["pi"], ["bi"])
-        if t == 0:
-            ts(T.kq[:, 15:K:16], T.kq[:, 15:K:16], -8.0 / MID, None, A.add, None, ["kq"], ["kq"])
+        resets((6, 7, 8))
         cp(T.abu[:, 0:2 * KB], T.abi[:, 0:2 * KB], ["ai", "bi"], ["abu"])
         if t == 0:
             quant("gq", 128, 384, T.gt[:, 512:1536], ["gt1", "gt2"], "gq2")
@@ -382,13 +403,13 @@ def rank_program(g, core, T, topo):
         cp(T.dtile[:, 0:4 * K:4], T.sg[:].indirect(T.abu[:, 0:KB]), ["sg", "abu"], ["dt0"])
         act(T.dtile[:, 1:4 * K:4], T.sg[:].indirect(T.abu[:, KB:2 * KB]), F.Copy, ["sg", "abu"], ["dt1"])
         for b in range(4):
-            if t == 0 and b >= 2:
-                half(b)
             act(T.rg[:, K * b:K * b + K], T.th[:, C * b:C * b + C].indirect(T.abu[:, KB:2 * KB]), F.Copy,
                 ["th%d" % b, "abu"], ["rg%d" % b])
         if t == 0:
             tt(T.oo[:, 32:32 + KB], T.abi[:, 0:KB], T.abi[:, KB:2 * KB], A.subtract, ["ai", "bi"], ["dd"])
             act(T.ownb[:, 16:32], T.jw[:, 0:16], F.Identity, ["jw"], ["dump"], scale=4.0, bias=320.0)
+            nobody()
+            whole()
         quant("dq", 0, K, T.dtile[:], ["dt0", "dt1"])
         mm(7, "gq", 128, "dq", K, extra=["gq2"])
         mm(1, "gq", 256, "dq", K, extra=["gq2"])
@@ -409,42 +430,30 @@ def rank_program(g, core, T, topo):
         cp(T.lru[:, 0:2 * KB], T.lr[:, 0:2 * KB], ["lf", "rf"], ["lru"])
         act(T.ownb[:, 0:KB], T.lr[:, 0:KB], F.Identity, ["lf"], ["ownb"], bias=-144.0)
         act(T.rowf[:], T.iota[:].indirect(T.lru[:, 0:KB]), F.Identity, ["iota", "lru"], ["rowf"], bias=-144.0)
+        if last:
+            act(T.r1[:], T.iota[:].indirect(T.lru[:, 0:2 * KB]), F.Copy, ["iota", "lru"], ["r1"])
         pack(2)
         pack(3)
-        if t == 0:
-            for c in range(KB):
-                if c < 4:
-                    act(T.dr[:, SEG[c] + 1:SEG[c] + 17], T.m01[:, 0:16], F.Identity, ["m01", "dra", "drb"], ["dr%d" % c],
-                        scale=-1.0, bias=1.0)
-                else:
-                    ts(T.dr[:, SEG[c] + 1:SEG[c] + 17], T.m01[:, 0:16], -1.0, 1.0, A.mult, A.add, ["m01", "dra", "drb"],
-                       ["dr%d" % c])
-                if c == 5:
-                    quant("mq", 0, K, T.mt[:], ["mt0", "mt1", "mt2", "mt3"])
-        else:
-            repeats(KB - 1)
-            quant("mq", 0, K, T.mt[:], ["mt0", "mt1", "mt2", "mt3"])
+        quant("mq", 0, K, T.mt[:], ["mt0", "mt1", "mt2", "mt3"])
         need("t", ("w%d" % t, _arrivals(T, topo, rank, t)))
         for b in range(4):
             mm(2 + b, "wl%d" % t, 128 * b, "mq", K)
             act(T.ht[:, b:4 * K:4], ps(2 + b, 0, K), F.Copy, ["ps%d" % (2 + b)], ["ht%d" % b], scale=0.03125)
         for b in (2, 3):
             mm(b, "eq", 128 * b, "xq", C)
-        for c in range(KB if t == 0 else KB - 1):
+        if last:
+            act(T.r2[:], T.r1[:].indirect(T.revu[:, 0:2 * KB]), F.Copy, ["r1", "rev0", "rev1"], ["r2"])
+            dma("y", T.ol[:], T.r2[0:128:16, :], ["r2"], [])
+        for c in range(KB):
             repeats(c)
-        if t == 0:
-            nobody()
-            act(T.klow[:], T.kbig[:], F.Copy, ["kbig"], ["klow"], scale=LOW / LIFT)
-        scan(T.fl[:], T.dr[:], T.ee[:], 0.0, A.mult, A.max,
-             ["ee%d" % c for c in range(KB)] + ["dr%d" % c for c in range(KB)], ["fl"])
+        repeated(0, 6)
+        repeated(6, KB)
+        tt(T.oo[:, 0:16], T.fl[:].indirect(T.endu[:, 0:1]), T.lr[:, 0:16], A.max, ["fl0", "fl6", "endu", "lf", "rf"], ["o1"])
         quant("rq", 0, K, T.ht[:], ["ht0", "ht1", "ht2", "ht3"])
         for b in range(4):
             bank = (0, 1, 6, 7)[b]
             mm(bank, "eq", 128 * b, "rq", K)
             act(T.dh[:, DW * b:DW * b + K], ps(bank, 0, K), F.Copy, ["ps%d" % bank], ["dh%d" % b])
-            if t == 0 and b == 1:
-                whole()
-        tt(T.oo[:, 0:16], T.fl[:].indirect(T.endu[:, 0:1]), T.lr[:, 0:16], A.max, ["fl", "endu", "lf", "rf"], ["o1"])
         cp(T.su[:, 0:KB], T.oo[:, 0:KB], ["o1"], ["su"])
         cp(T.who[:].indirect(T.su[:, 0:KB]), T.iota[:, 0:K], ["su", "iota"], ["who"])
         scan(T.whs[:], T.who[:, 0:C], T.klow[:], -LOW, A.max, A.add, ["who", "klow"], ["whs"])
@@ -455,26 +464,20 @@ def rank_program(g, core, T, topo):
         for b in (0, 1):
             tt(T.xt[:, b:4 * C:4], T.dh[:, DW * b:DW * b + K + 1].indirect(T.wu[:, 0:CB]), T.tp[:, C * b:C * b + C], A.add,
                ["dh%d" % b, "dhz", "wu", "tp"], ["xt%d" % b])
-        if last:
-            act(T.r1[:], T.iota[:].indirect(T.lru[:, 0:2 * KB]), F.Copy, ["iota", "lru"], ["r1"])
-            act(T.r2[:], T.r1[:].indirect(T.revu[:, 0:2 * KB]), F.Copy, ["r1", "rev0", "rev1"], ["r2"])
-            dma("y", T.ol[:], T.r2[0:128:16, :], ["r2"], [])
         for b in (2, 3):
             tt(T.xt[:, b:4 * C:4], ps(b, 0, C), T.gd[:, C * (b - 2):C * (b - 1)], A.add, ["ps%d" % b, "gd%d" % b],
                ["xt%d" % b])
 
     quant("xq", 0, C, T.xt[:], XT)
-    H = C // 2
     mm(0, "vq", 0, "xq", H)
     mm(1, "vq", 0, "xq", H, x0=H)
     dma("y", T.oc[:], T.xq[:].bitcast(dt.uint8), ["xq"], [])
+    for k in range(4):
+        dma("y" if k % 2 else "s", T.osc[4 * k:4 * k + 4, :], T.xqs[32 * k:32 * k + 4, :], ["xq"], [])
     cp(T.yt[:, 0:H], ps(0, 0, H), ["ps0"], ["yt0"])
-    dma("s", T.osc[0:4, :], T.xqs[0:4, :], ["xq"], [])
     act(T.yt[:, H:C], ps(1, 0, H), F.Copy, ["ps1"], ["yt1"])
-    dma("y", T.osc[4:8, :], T.xqs[32:36, :], ["xq"], [])
-    dma("y", T.y[:], T.yt[:], ["yt0", "yt1"], [])
-    for k in (2, 3):
-        dma("s", T.osc[4 * k:4 * k + 4, :], T.xqs[32 * k:32 * k + 4, :], ["xq"], [])
+    dma("y", T.y[:, 0:H], T.yt[:, 0:H], ["yt0"], [])
+    dma("s", T.y[:, H:C], T.yt[:, H:C], ["yt1"], [])
 
     g.wait_ge(T.sem.hout, 8 * share)
     need("g", ("cg", count["g"]))

@@ -4,13 +4,16 @@ from concourse.mybir import dt, AluOpType, ActivationFunctionType
 C, K, R = 288, 160, 3
 CB, KB = C // 16, K // 16
 H = C // 2
+NS = 2
 BIG = 2.0 ** 96
 TINY = 2.0 ** -120
-LIFT, MID, LOW = 2.0 ** 20, 2.0 ** 12, 256.0
-ST = [0, 64, 128, 160, 160]
+LIFT, MID, LOW = 2.0 ** 20, 2.0 ** 12, 512.0
+TW = [288, 224, 160, 160]
+LO = 128
 SEG = [176 * c - 8 * c * c for c in range(KB + 1)]
-DW = 176
+PW = C + K
 RISE = (1.0 / 32, 0.5, 8.0, 128.0)
+DB = (0, 1, 6, 7)
 Q8, U8, BF, F32, I32, U16 = "float8_e4m3fn_x4", "uint8", "bfloat16", "float32", "int32", "uint16"
 
 SCRATCH = {}
@@ -21,21 +24,21 @@ def _sb(name, n, d):
 
 
 for _n, _w in (("wq", 512), ("hq", 128), ("wl0", 512), ("wl1", 512), ("wl2", 512), ("xq", C), ("uq", 128), ("ub", 128),
-               ("vq", 128), ("eq", 512), ("gq", 384), ("zq", 160), ("dq", K), ("mq", K), ("rq", K),
-               ("cq0", C), ("cq1", C), ("cq2", C), ("cq3", C), ("cq4", C)):
+               ("vq", 128), ("eq", 512), ("gq", 384), ("zq", 128), ("dq", K), ("mq", K), ("rq", K),
+               ("cq0", C), ("cq1", C), ("cq2", C), ("cq3", C)):
     _sb(_n, _w, Q8)
     _sb(_n + "s", _w, U8)
 for _n, _w in (("xt", 4 * C), ("ut", 512), ("vt", 512), ("et", 2048), ("gt", 1536), ("ones", 512), ("zt", 640),
-               ("srow", C), ("m01", C), ("m1", C), ("r01", C), ("rst", C), ("sg", C), ("th", 4 * C),
-               ("tp", 2 * C), ("gd", 2 * C), ("junk", 2448), ("cd", C), ("dtile", 4 * K), ("rg", 8 * K), ("mt", 4 * K),
-               ("ht", 4 * K), ("dh", 4 * DW), ("rowf", K), ("ownb", 32), ("ee", 960), ("dr", 960), ("fl", 960),
-               ("who", 960), ("whs", C), ("kbig", C), ("klow", C), ("kmid", K)):
+               ("srow", H), ("m01", H), ("m1", H), ("cdr", C), ("rst", H), ("sg", C), ("th", 4 * PW), ("sr", NS * C),
+               ("pm", 2 * K), ("two", 4 * K), ("tl", 4 * K), ("junk", 2448), ("cd", C), ("dtile", 4 * K), ("rg", 6 * K),
+               ("mt", 4 * K), ("ht", 4 * K), ("rowf", K), ("ownb", 32), ("ee", 960), ("dr", 960),
+               ("fl", 960), ("who", 960), ("kbig", C), ("klow", C), ("kmid", K)):
     _sb(_n, _w, BF)
-for _t in range(5):
-    _sb("ct%d" % _t, 4 * (C - ST[_t]), BF)
+for _t in range(4):
+    _sb("ct%d" % _t, 4 * TW[_t], BF)
 for _n, _w in (("iota", C), ("lrow", C), ("lm", C), ("bm", C), ("lat", C), ("srt", C), ("pa", C), ("pb", C),
                ("pw", C), ("qf", 8), ("col", 16), ("jw", 96), ("blk", 32), ("rows", 32), ("zz", 96),
-               ("lr", 32), ("oo", 96), ("r1", 2 * K), ("r2", 2 * K), ("yt", C), ("kcol", C), ("kq", K)):
+               ("lr", 32), ("oo", 96), ("r1", 2 * K), ("r2", 2 * K), ("yt", C), ("whs", C), ("kcol", C), ("kq", K)):
     _sb(_n, _w, F32)
 for _n, _w in (("li", CB), ("mi", CB), ("pi", 16), ("abi", 32), ("fi", 32), ("ci", 16), ("gi", 32)):
     _sb(_n, _w, I32)
@@ -156,6 +159,12 @@ def rank_program(g, core, T, topo):
     def cp(out, in_, r, w):
         op("v", lambda: V.tensor_copy(out, in_), r, w)
 
+    def fill(out, c, w):
+        op("v", lambda: V.memset(out, c), [], w)
+
+    def iota(out, pattern, base, w):
+        op("g", lambda: g.iota(out, pattern, base, 0, allow_small_or_imprecise_dtypes=True), [], w)
+
     def scan(out, d0, d1, init, o0, o1, r, w):
         op("v", lambda: V.tensor_tensor_scan(out, d0, d1, init, o0, o1), r, w)
 
@@ -185,31 +194,47 @@ def rank_program(g, core, T, topo):
         act(T.col[:, 9:10], T.col[:, 8:9], F.Copy, ["col8"], ["col9"], scale=-1.0)
 
     def tiles():
-        act(T.gt[:, 1024:1536], T.gt[:, 0:512], F.Copy, ["gt0", "col7"], ["gt2"], scale=T.col[:, 7:8])
-        act(T.gt[:, 512:1024], T.ones[:], F.Copy, ["ones", "col8"], ["gt1"], scale=T.col[:, 8:9])
-        act(T.gt[:, 1025:1536:4], T.gt[:, 0:512:4], F.Copy, ["gt0", "col10"], ["gt2"], scale=T.col[:, 10:11])
-        act(T.gt[:, 513:1024:4], T.ones[:, 0:128], F.Copy, ["ones", "col9"], ["gt1"], scale=T.col[:, 9:10])
+        act(T.gt[:, 1024:1536:4], T.gt[:, 0:512:4], F.Copy, ["gt0", "col10", "gz2"], ["gt2a"], scale=T.col[:, 10:11])
+        act(T.gt[:, 512:1024:4], T.ones[:, 0:128], F.Copy, ["ones", "col8", "gz1"], ["gt1a"], scale=T.col[:, 8:9])
+        act(T.gt[:, 1025:1536:4], T.gt[:, 0:512:4], F.Copy, ["gt0", "col7", "gz2"], ["gt2b"], scale=T.col[:, 7:8])
+        act(T.gt[:, 513:1024:4], T.ones[:, 0:128], F.Copy, ["ones", "col9", "gz1"], ["gt1b"], scale=T.col[:, 9:10])
 
     def planes():
-        for b in range(4):
+        for b in (2, 3, 0, 1):
             mm(2 + b, "eq", 128 * b, "xq", C)
 
-    def half(b):
-        act(T.th[:, C * b:C * b + C], ps(2 + b, 0, C), F.Copy, ["ps%d" % (2 + b)], ["th%d" % b], scale=0.5)
+    def held(b, n=C):
+        return T.th[:, PW * b:PW * b + n]
 
-    def whole():
-        act(T.tp[:], T.th[:, 0:2 * C], F.Copy, ["th0", "th1"], ["tp"], scale=2.0)
+    def plane(b):
+        act(held(b), ps(2 + b, 0, C), F.Copy, ["ps%d" % (2 + b)], ["th%d" % b])
 
-    def nobody():
-        act(T.who[:, 0:C], T.srow[:], F.Identity, ["srow"], ["who"], scale=0.0, bias=float(K))
+    def first(b):
+        act(T.rg[:, K * b:K * b + K], held(b).indirect(T.abu[:, 0:KB]), F.Copy, ["th%d" % b, "au"], ["rg%d" % b])
 
     def diff(b):
-        tt(T.rg[:, K * (4 + b):K * (5 + b)], T.th[:, C * b:C * b + C].indirect(T.abu[:, 0:KB]), T.rg[:, K * b:K * b + K],
-           A.subtract, ["th%d" % b, "abu", "rg%d" % b], ["df%d" % b])
+        out = T.rg[:, K * (4 + b):K * (5 + b)] if b < 2 else T.two[:, 2 * K * (b - 2) + 1:2 * K * (b - 1):2]
+        tt(out, held(b).indirect(T.abu[:, KB:2 * KB]), T.rg[:, K * b:K * b + K], A.subtract,
+           ["th%d" % b, "bu", "rg%d" % b], ["df%d" % b])
+
+    def turn(b):
+        act(T.two[:, 2 * K * (b - 2):2 * K * (b - 1):2], T.two[:, 2 * K * (b - 2) + 1:2 * K * (b - 1):2], F.Copy,
+            ["df%d" % b], ["dn%d" % b], scale=-1.0)
 
     def pack(b):
-        tt(T.mt[:, b:4 * K:4], T.blk[:, 24:26].indirect(T.su[:, 16:16 + KB]), T.rg[:, K * (4 + b):K * (5 + b)], A.mult,
-           ["pm0", "pm1", "fu", "df%d" % b], ["mt%d" % b])
+        if b < 2:
+            tt(T.mt[:, b:4 * K:4], T.pm[:].indirect(T.su[:, 16:16 + KB]), T.rg[:, K * (4 + b):K * (5 + b)], A.mult,
+               ["pm0", "pm1", "fu", "df%d" % b], ["mt%d" % b])
+        else:
+            act(T.mt[:, b:4 * K:4], T.two[:, 2 * K * (b - 2):2 * K * (b - 1)].indirect(T.su[:, 16:16 + KB]), F.Copy,
+                ["fu", "df%d" % b, "dn%d" % b], ["mt%d" % b], scale=0.5)
+
+    def left(b):
+        act(T.tl[:, K * b:K * b + K], held(b).indirect(T.lru[:, 0:KB]), F.Copy, ["th%d" % b, "lru"], ["tl%d" % b])
+
+    def renew(b):
+        tt(T.th[:, PW * b + C:PW * b + PW], ps(DB[b], 0, K), T.tl[:, K * b:K * b + K], A.add,
+           ["ps%d" % DB[b], "tl%d" % b], ["new%d" % b])
 
     def repeats(c):
         ts(T.ee[:, SEG[c]:SEG[c] + K - 16 * c], T.rowf[:, 16 * c:K], T.ownb[:, c:c + 1], T.ownb[:, 16 + c:17 + c],
@@ -219,37 +244,82 @@ def rank_program(g, core, T, topo):
         scan(T.fl[:, SEG[c0]:SEG[c1]], T.dr[:, SEG[c0]:SEG[c1]], T.ee[:, SEG[c0]:SEG[c1]], 0.0, A.mult, A.max,
              ["ee%d" % c for c in range(c0, c1)] + ["dr%d" % c for c in range(c0, c1)], ["fl%d" % c0])
 
+    def line(c):
+        s = CB - c
+        tau, e, a = min(s // 4, 3), s % 4, LO * (s // 16)
+        return T["ct%d" % tau][:, 4 * a + e:4 * (a + 16 * c):4]
+
+    def lines(tau):
+        return ["c%d" % c for c in (range(CB - 4 * tau - 3, CB - 4 * tau + 1) if tau < 3 else range(1, 7))]
+
+    def own(c):
+        return T.lat[:, 16 * c + 15:16 * c + 16]
+
+    def compare(c):
+        ts(line(c), ps(0, 0, 16 * c), own(c), None, A.is_lt, None, ["ps0", "lat%d" % (16 * c // H)], ["c%d" % c])
+        jo = 8 * c * (c - 1)
+        act(T.junk[:, jo:jo + 16 * c], line(c), F.Copy, ["c%d" % c], ["junk%d" % c, "row%d" % c],
+            accum_out=T.rows[:, c:c + 1])
+
     def sums(tau):
-        quant("cq%d" % tau, ST[tau], C, T["ct%d" % tau][:], ["c%d" % x for x in range(4 * tau, 4 * tau + 4)])
-        mm(6, "gq", 0, "cq%d" % tau, C, tau == 0, tau == 4, extra=["cqh%d" % tau, "cqi%d" % tau])
+        quant("cq%d" % tau, 0, TW[tau], T["ct%d" % tau][:], lines(tau))
+        extra = ["cqh%d" % tau, "cqi%d" % tau]
+        if tau < 3:
+            mm(7, "gq", 0, "cq%d" % tau, C - LO, tau == 0, tau == 2, extra=extra, x0=LO)
+            mm(6, "gq", 0, "cq%d" % tau, LO, tau == 0, False)
+        else:
+            mm(6, "gq", 0, "cq3", LO, False, False)
+            mm(6, "gq", 0, "cq3", LO, False, True, extra=extra, x0=LO)
+
+    def terms(h):
+        a, b = (0, LO // 16) if h == 0 else (LO // 16, CB)
+        tt(T.kcol[:, 16 * a + 15:16 * b:16], T.zz[:, 32 + a:32 + b], T.rows[:, a:b], A.add,
+           ["z2", "rowz"] + ["row%d" % c for c in range(max(a, 1), b)], ["kcol%d" % h])
+
+    def places(h):
+        a, b = (0, LO) if h == 0 else (LO, C)
+        scan(T.pw[:, a:b], ps(6 + h, 0, b - a), T.kcol[:, a:b], -LIFT, A.max, A.add, ["ps%d" % (6 + h), "kcol%d" % h],
+             ["pw%d" % h])
+
+    def offsets(h):
+        a, b = (0, LO // 16) if h == 0 else (LO // 16, CB)
+        ts(T.ru[:, a:b], T.pw[:, 16 * a + 15:16 * b:16], LIFT, None, A.add, None, ["pw%d" % h], ["ru%d" % h])
+
+    def spread(h):
+        a, b = (0, LO // 16) if h == 0 else (LO // 16, CB)
+        cp(T.srt[:].indirect(T.ru[:, a:b]), T.lm[:, 16 * a:16 * b], ["ru%d" % h, "lm"], ["srt"])
 
     XT = ["xt0", "xt1", "xt2", "xt3"]
-    dma("y", T.xt[:], T.x[:], [], XT)
     dma("s", T.ut[:], T.u[:], [], ["ut"])
-    dma("y", T.wq[:].bitcast(dt.uint8), T.wc[:], [], ["wq"])
-    dma("s", T.wqs[:], T.ws[:], [], ["wqs"])
+    dma("y", T.xt[:], T.x[:], [], XT)
     dma("y", T.li[:], T.l[:], [], ["li"])
     dma("y", T.mi[:], T.m[:], [], ["mi"])
+    dma("y", T.wq[:].bitcast(dt.uint8), T.wc[:], [], ["wq"])
+    dma("y", T.wqs[:], T.ws[:], [], ["wqs"])
 
     q = T.qf[:, 0:1]
-    op("v", lambda: V.memset(T.zt[:], 0.0), [], ["zt"])
-    op("v", lambda: V.memset(T.ones[:], 1.0), [], ["ones"])
+    fill(T.zt[:], 0.0, ["zt"])
+    fill(T.ones[:], 1.0, ["ones"])
     op("g", lambda: g.iota(T.ci[:, 0:1], [[0, 1]], 0, 1), [], ["ci0"])
-    op("g", lambda: g.iota(T.jw[:, 0:20], [[16, 20]], 0, 0, allow_small_or_imprecise_dtypes=True), [], ["jw"])
-    op("g", lambda: g.iota(T.srow[:], [[0, CB], [1, 16]], 0, 0, allow_small_or_imprecise_dtypes=True), [], ["srow"])
+    iota(T.jw[:, 0:20], [[16, 20]], 0, ["jw"])
+    iota(T.srow[:], [[0, H // 16], [1, 16]], 0, ["srow"])
     op("g", lambda: g.iota(T.gi[:], [[1, 8], [0, 4]], 0, 0), [], ["gi"])
-    op("g", lambda: g.iota(T.blk[:, 24:26], [[-2, 2]], 1, 0, allow_small_or_imprecise_dtypes=True), [], ["pm0", "pm1"])
-    op("g", lambda: g.iota(T.iota[:], [[1, C]], 0, 0, allow_small_or_imprecise_dtypes=True), [], ["iota"])
+    iota(T.iota[:], [[1, C]], 0, ["iota"])
+    iota(T.cdr[:], [[0, C]], 256, ["cdr"])
+    iota(T.cdr[:, 0:C:16], [[-16, CB]], H, ["cdr"])
 
-    for t in range(5):
-        n = (192, 192, 192, 320, 512)[t]
-        act(T["ct%d" % t][:, 0:n], T.zt[:, 0:n], F.Copy, ["zt"], ["c%d" % s for s in range(4 * t, 4 * t + 4)])
+    for t in range(4):
+        n = (192, 192, 192, 448)[t]
+        act(T["ct%d" % t][:, 4 * TW[t] - n:4 * TW[t]], T.zt[:, 0:n], F.Copy, ["zt"], lines(t))
     for b in range(4):
         dma("y", T.et[:, 512 * b:512 * b + 512], T.zt[:, 0:512], ["zt"], ["et%d" % b])
-    quant("zq", 0, 160, T.zt[:], ["zt"])
-    for t in range(1, 5):
-        dma("y", T["cq%d" % t][:, 0:ST[t]].bitcast(dt.uint8), T.zq[:, 0:ST[t]].bitcast(dt.uint8), ["zq"], ["cqh%d" % t])
-        dma("y", T["cq%ds" % t][:, 0:ST[t]], T.zqs[:, 0:ST[t]], ["zq"], ["cqi%d" % t])
+    quant("zq", 0, 128, T.zt[:, 0:512], ["zt"])
+    for t in range(1, 4):
+        n = C - TW[t]
+        dma("y", T["cq%d" % t][:, C - n:C].bitcast(dt.uint8), T.zq[:, 0:n].bitcast(dt.uint8), ["zq"], ["cqh%d" % t])
+        dma("y", T["cq%ds" % t][:, C - n:C], T.zqs[:, 0:n], ["zq"], ["cqi%d" % t])
+    dma("y", T.gt[:, 512:1024], T.zt[:, 0:512], ["zt"], ["gz1"])
+    dma("y", T.gt[:, 1024:1536], T.zt[:, 0:512], ["zt"], ["gz2"])
     dma("y", T.dtile[:], T.zt[:], ["zt"], ["dt0", "dt1"])
     dma("y", T.dr[:, 0:480], T.ones[:, 0:480], ["ones"], ["dra"])
     dma("y", T.dr[:, 480:960], T.ones[:, 0:480], ["ones"], ["drb"])
@@ -260,30 +330,25 @@ def rank_program(g, core, T, topo):
     ts(T.ci[:, 1:2], T.ci[:, 0:1], 15, None, A.bitwise_and, None, ["ci0"], ["ci1"])
     cp(T.qf[:, 1:2], T.ci[:, 0:1], ["ci0"], ["p"])
     cp(T.pu[:, 0:8], T.jw[:, 0:8], ["jw"], ["pu"])
-    op("v", lambda: V.memset(T.rows[:, CB - 1:CB], 0.0), [], ["rowz"])
+    fill(T.rows[:, 0:1], 0.0, ["rowz"])
     cp(q, T.ci[:, 1:2], ["ci1"], ["q"])
-    op("v", lambda: V.memset(T.dh[:, K:4 * DW:DW], 0.0), [], ["dhz"])
-    ts(T.r01[:], T.srow[:], 0.0, None, A.not_equal, None, ["srow"], ["r01"])
+    ts(T.rst[:], T.srow[:], 2 * BIG, -BIG, A.mult, A.add, ["srow"], ["rst"])
+    cp(T.gu[:], T.gi[:], ["gi"], ["gu"])
     ts(T.jw[:, 0:20], T.jw[:, 0:20], q, None, A.add, None, ["jw", "q"], ["jw"])
     ts(T.m01[:], T.srow[:], q, None, A.is_equal, None, ["srow", "q"], ["m01"])
-    ts(T.qf[:, 2:3], q, 1.0, float(KB), A.add, A.min, ["q"], ["e0"])
-    cp(T.gu[:], T.gi[:], ["gi"], ["gu"])
-    ts(T.blk[:, 16:24], T.jw[:, 0:8], T.qf[:, 1:2], None, A.is_equal, None, ["jw", "p"], ["gb"])
     ts(T.zz[:, 0:16], T.srow[:, 0:16], q, -1.0, A.is_lt, A.mult, ["srow", "q"], ["z1"])
+    ts(T.blk[:, 16:24], T.jw[:, 0:8], T.qf[:, 1:2], None, A.is_equal, None, ["jw", "p"], ["gb"])
     ts(T.qu[:, 0:CB], T.zt[:, 0:CB], q, None, A.add, None, ["zt", "q"], ["qu"])
-    ts(T.qf[:, 3:4], T.qf[:, 2:3], -8.0, 176.0, A.mult, A.add, ["e0"], ["e1"])
-    ts(T.rst[:], T.r01[:], 2 * BIG, BIG, A.mult, A.subtract, ["r01"], ["rst"])
     tt(T.blk[:, 0:16], T.zz[:, 0:16], T.m01[:, 0:16], A.add, ["z1", "m01"], ["kb"])
-    ts(T.m1[:], T.m01[:], 2 * BIG, BIG, A.mult, A.subtract, ["m01"], ["m1"])
-    ts(T.qf[:, 4:5], T.qf[:, 3:4], T.qf[:, 2:3], 1.0, A.mult, A.subtract, ["e0", "e1"], ["e2"])
+    ts(T.m1[:], T.m01[:], 2 * BIG, -BIG, A.mult, A.add, ["m01"], ["m1"])
     ts(T.blk[:, 15:16], T.blk[:, 15:16], -2.0, None, A.add, None, ["kb"], ["kb"])
-    act(T.gt[:, 0:512], T.blk[:, 16:24].indirect(T.gu[:]), F.Copy, ["gb", "gu"], ["gt0"])
+    act(T.gt[:, 0:512], T.blk[:, 16:24].indirect(T.gu[:]), F.Copy, ["gb", "gu"], ["gt0"], scale=-1.0)
 
     quant("uq", 0, 128, T.ut[:], ["ut"])
-    cp(T.endu[:, 0:1], T.qf[:, 4:5], ["e2"], ["endu"])
+    ts(T.qf[:, 2:3], q, 1.0, float(KB), A.add, A.min, ["q"], ["e0"])
     cp(T.ub[:].bitcast(dt.uint32), T.uq[:].bitcast(dt.uint32).indirect(T.pu[:, 0:8]), ["uq", "pu"], ["ub"])
     act(T.ubs[:], T.uqs[:].indirect(T.pu[:, 0:8]), F.Copy, ["uq", "pu"], ["ubs"])
-    weights()
+    act(T.kcol[:], T.blk[:, 0:16].indirect(T.qu[:, 0:CB]), F.Copy, ["kb", "qu"], ["kcol0", "kcol1"], scale=LIFT)
 
     hs = _helpers(T, topo, rank)
     eng = topo.engines(core, hs[0])
@@ -300,173 +365,193 @@ def rank_program(g, core, T, topo):
                                          dma_engine_mask=_bits(eng[share * b:share * b + share]),
                                          remote_sem=T.sem.hin, src=src, dst=dst))
         g.remote_dma_fused(trs, local_sem=T.sem.hout)
-    for b in range(4):
+    for b in (2, 3, 0, 1):
         op("g", lambda: g.affine_select(T.et[:, 512 * b + b:512 * b + 512:4], T.ones[:, 0:128], [[-1, 128]], A.is_equal,
                                         0.0, 0, 1), ["ones"], ["et%d" % b])
 
+    def resets(cs):
+        for c in cs:
+            ts(T.dr[:, SEG[c] + 1:SEG[c] + 17], T.m01[:, 0:16], -1.0, 1.0, A.mult, A.add, ["m01", "dra", "drb"],
+               ["dr%d" % c])
+
+    later = [
+        lambda: ts(T.kbig[:, 0:K], T.kcol[:, 0:K], 1.0, None, A.mult, None, ["kcol0", "kcol1"], ["kbig"]),
+        lambda: tt(T.lm[:], T.iota[:].indirect(T.mu[:, 0:CB]), T.lrow[:], A.add, ["iota", "mu", "lrow"], ["lm"]),
+        lambda: ts(T.kmid[:], T.kbig[:, 0:K], MID / LIFT, None, A.mult, None, ["kbig"], ["kmid"]),
+        lambda: ts(T.kq[:], T.kbig[:, 0:K], MID / LIFT, None, A.mult, None, ["kbig"], ["kq"]),
+        lambda: (ts(T.kq[:, 15:K:16], T.kq[:, 15:K:16], -8.0 / MID, None, A.add, None, ["kq"], ["kq"]),
+                 ts(T.qf[:, 3:4], T.qf[:, 2:3], -8.0, 176.0, A.mult, A.add, ["e0"], ["e1"])),
+        lambda: (fill(T.pm[:, 0:2 * K:2], -0.5, ["pm0"]), fill(T.pm[:, 1:2 * K:2], 0.5, ["pm1"])),
+        lambda: (ts(T.qf[:, 4:5], T.qf[:, 3:4], T.qf[:, 2:3], 1.0, A.mult, A.subtract, ["e0", "e1"], ["e2"]),
+                 ts(T.jw[:, 64:64 + KB], T.jw[:, 0:KB], 2.0, None, A.mult, None, ["jw"], ["jw2"])),
+        lambda: quant("gq", 128, 384, T.gt[:, 512:1536], ["gt1a", "gt1b", "gt2a", "gt2b"], "gq2"),
+    ]
+
     for t in range(R):
         last = t == R - 1
+
+        def slot(i):
+            if t == 0:
+                later[i]()
+
         quant("xq", 0, C, T.xt[:], XT)
         mm(0, "ub", 0, "xq", C, extra=["ubs"])
+        mm(7, "ub", 0, "xq", C, extra=["ubs"])
         mm(1, "uq", 0, "xq", C)
         if t == 0:
             quant("gq", 0, 128, T.gt[:, 0:512], ["gt0"])
             cp(T.lu[:, 0:CB], T.li[:], ["li"], ["lu"])
             cp(T.mu[:, 0:CB], T.mi[:], ["mi"], ["mu"])
+            ts(T.qf[:, 5:6], T.blk[:, 15:16], LIFT, float(C - 16 - H), A.mult, A.add, ["kb"], ["k0"])
         else:
             planes()
+        iota(T.who[:, 0:C], [[1, C]], -PW // 2, ["who"])
         if t == 1:
             quant("vq", 0, 128, T.vt[:], ["vt"])
         if last:
             ts(T.revu[:, 0:KB], T.jw[:, 0:KB], -1.0, float(K - 1), A.mult, A.add, ["jw"], ["rev0"])
             ts(T.revu[:, KB:2 * KB], T.jw[:, KB:2 * KB], -1.0, float(3 * K - 1), A.mult, A.add, ["jw"], ["rev1"])
-        for h in range(2):
+        for h in (1, 0):
             tt(T.bm[:, H * h:H * h + H], ps(0, H * h, H * h + H), T.m1[:, 0:H], A.min, ["ps0", "m1"], ["bm%d" % h])
-        for h in range(2):
+        for h in (1, 0):
             scan(T.lat[:, H * h:H * h + H], T.rst[:, 0:H], T.bm[:, H * h:H * h + H], -BIG, A.min, A.max,
                  ["rst", "bm%d" % h], ["lat%d" % h])
-        if t > 0:
-            act(T.sg[:], ps(1, 0, C), F.Sign, ["ps1"], ["sg"], bias=-TINY)
-            half(0)
-        else:
-            act(T.kbig[:], T.blk[:, 0:16].indirect(T.qu[:, 0:CB]), F.Copy, ["kb", "qu"], ["kbig"], scale=LIFT)
-        jo = 0
-        for s in (1, 0) + tuple(range(2, CB)):
-            tau, e = s // 4, s % 4
-            tile = T["ct%d" % tau]
-            if s == 0:
-                tt(tile[:, 0:4 * C:4], ps(0, 0, C), T.lat[:], A.is_le, ["ps0", "lat0", "lat1"], ["c0"])
-            else:
-                c = s - 1
-                a = 16 * c + 16
-                view = tile[:, 4 * (a - ST[tau]) + e:4 * (C - ST[tau]):4]
-                ts(view, ps(0, a, C), T.lat[:, 16 * c + 15:16 * c + 16], None, A.is_le, None,
-                   ["ps0", "lat%d" % (16 * c // H)], ["c%d" % s])
-                act(T.junk[:, jo:jo + C - a], view, F.Copy, ["c%d" % s], ["junk%d" % c, "row%d" % c],
-                    accum_out=T.rows[:, c:c + 1])
-                jo += C - a
-            if t == 0 and s == 1:
-                act(T.kcol[:], T.kbig[:], F.Copy, ["kbig"], ["kcol"])
-            if t == 0 and s == 9:
-                tt(T.jw[:, 32:32 + CB], T.kbig[:, 15:C:16], T.jw[:, 0:CB], A.subtract, ["kbig", "jw"], ["kc"])
-            if s in (4, 9, 14, 17):
-                sums((4, 9, 14, 17).index(s))
-        scan(T.cd[:], T.r01[:], T.ct0[:, 0:4 * C:4], 0.0, A.mult, A.add, ["r01", "c0"], ["cd"])
-        sums(4)
+        if t == 0:
+            act(T.klow[:], T.kcol[:], F.Copy, ["kcol0", "kcol1"], ["klow"], scale=LOW / LIFT)
+        for i in range(NS):
+            c = CB - 1 - i
+            act(T.sr[:, C * i:C * i + 16 * c], ps(7, 0, 16 * c), F.Sign, ["ps7", "lat1"], ["sr%d" % c],
+                scale=-1.0, bias=own(c))
+        for i in range(NS):
+            c = CB - 1 - i
+            act(line(c), T.sr[:, C * i:C * i + 16 * c], F.Relu, ["sr%d" % c], ["c%d" % c, "row%d" % c],
+                accum_out=T.rows[:, c:c + 1])
+        compare(CB - 1 - NS)
+        if t == 0:
+            tt(T.qf[:, 6:7], T.qf[:, 5:6], q, A.add, ["k0", "q"], ["k1"])
+        tt(T.ct0[:, 0:4 * C:4], ps(0, 0, C), T.lat[:], A.is_le, ["ps0", "lat0", "lat1"], ["c%d" % CB])
+        for c in range(CB - 2 - NS, 0, -1):
+            compare(c)
+            if c == 13:
+                scan(T.cd[:], T.cdr[:], T.ct0[:, 0:4 * C:4], 256.0, A.min, A.add, ["cdr", "c%d" % CB], ["cd"])
+            if c in (11, 9, 5):
+                sums((11, 9, 5).index(c))
+            if c == 9:
+                act(T.zz[:, 32:32 + CB], T.cd[:, 15:C:16], F.Identity, ["cd", "k1"], ["z2"], bias=T.qf[:, 6:7])
+            if c == 3:
+                slot(0)
         if t == 0:
             act(T.lrow[:], T.iota[:].indirect(T.lu[:, 0:CB]), F.Copy, ["iota", "lu"], ["lrow"], scale=1024.0)
-        tt(T.zz[:, 32:32 + CB], T.jw[:, 32:32 + CB], T.cd[:, 15:C:16], A.subtract, ["cd", "kc"], ["z2"])
+        terms(1)
+        sums(3)
         if t == 0:
             quant("eq", 0, 512, T.et[:], ["et0", "et1", "et2", "et3"])
             planes()
-        tt(T.kcol[:, 15:C:16], T.zz[:, 32:32 + CB], T.rows[:, 0:CB], A.subtract,
-           ["z2", "rowz"] + ["row%d" % c for c in range(CB - 1)], ["kcol"])
+        places(1)
+        terms(0)
+        slot(1)
+        act(T.sg[:], ps(1, 0, C), F.Sign, ["ps1"], ["sg"], bias=-TINY)
         if t == 0:
-            ts(T.kmid[:], T.kbig[:, 0:K], MID / LIFT, None, A.mult, None, ["kbig"], ["kmid"])
-            ts(T.kq[:], T.kbig[:, 0:K], MID / LIFT, None, A.mult, None, ["kbig"], ["kq"])
-        scan(T.pw[:], ps(6, 0, C), T.kcol[:], -LIFT, A.max, A.add, ["ps6", "kcol"], ["pw"])
+            weights()
+        for b in (2, 3):
+            plane(b)
         if t == 0:
-            tt(T.lm[:], T.iota[:].indirect(T.mu[:, 0:CB]), T.lrow[:], A.add, ["iota", "mu", "lrow"], ["lm"])
             tiles()
-            act(T.sg[:], ps(1, 0, C), F.Sign, ["ps1"], ["sg"], bias=-TINY)
-            half(0)
-        for b in (1, 2, 3):
-            half(b)
-        ts(T.ru[:, 0:CB], T.pw[:, 15:C:16], -1.0, -LIFT, A.mult, A.add, ["pw"], ["ru"])
-        if t == 0:
-            ts(T.klow[:], T.kbig[:], LOW / LIFT, None, A.mult, None, ["kbig"], ["klow"])
-        cp(T.srt[:].indirect(T.ru[:, 0:CB]), T.lm[:], ["ru", "lm"], ["srt"])
-        if t > 0:
-            whole()
-            nobody()
-        else:
-            ts(T.kq[:, 15:K:16], T.kq[:, 15:K:16], -8.0 / MID, None, A.add, None, ["kq"], ["kq"])
-
-        def resets(cs):
-            for c in cs if t == 0 else ():
-                ts(T.dr[:, SEG[c] + 1:SEG[c] + 17], T.m01[:, 0:16], -1.0, 1.0, A.mult, A.add, ["m01", "dra", "drb"],
-                   ["dr%d" % c])
-
-        resets((9,))
+        for b in (0, 1):
+            plane(b)
+        offsets(1)
+        places(0)
+        spread(1)
+        slot(2)
+        offsets(0)
+        slot(3)
+        spread(0)
+        slot(4)
         scan(T.pa[:, 0:K], T.srt[:, C - K:C], T.kbig[:, 0:K], -LIFT, A.max, A.add, ["srt", "kbig"], ["pa"])
-        resets((0, 1, 2))
+        slot(5)
         ts(T.pi[:, 0:KB], T.pa[:, 15:K:16], LIFT, None, A.add, None, ["pa"], ["pi"])
-        resets((3, 4, 5))
-        ts(T.abi[:, 0:KB], T.pi[:, 0:KB], 10, None, A.arith_shift_right, None, ["pi"], ["ai"])
+        ts(T.abu[:, 0:KB], T.pa[:, 15:K:16], LIFT, 1.0 / 1024, A.add, A.mult, ["pa"], ["au"])
+        slot(6)
         ts(T.abi[:, KB:2 * KB], T.pi[:, 0:KB], 1023, None, A.bitwise_and, None, ["pi"], ["bi"])
-        resets((6, 7, 8))
-        cp(T.abu[:, 0:2 * KB], T.abi[:, 0:2 * KB], ["ai", "bi"], ["abu"])
-        if t == 0:
-            quant("gq", 128, 384, T.gt[:, 512:1536], ["gt1", "gt2"], "gq2")
-        else:
-            tt(T.oo[:, 32:32 + KB], T.abi[:, 0:KB], T.abi[:, KB:2 * KB], A.subtract, ["ai", "bi"], ["dd"])
-        cp(T.dtile[:, 0:4 * K:4], T.sg[:].indirect(T.abu[:, 0:KB]), ["sg", "abu"], ["dt0"])
-        act(T.dtile[:, 1:4 * K:4], T.sg[:].indirect(T.abu[:, KB:2 * KB]), F.Copy, ["sg", "abu"], ["dt1"])
-        for b in range(4):
-            act(T.rg[:, K * b:K * b + K], T.th[:, C * b:C * b + C].indirect(T.abu[:, KB:2 * KB]), F.Copy,
-                ["th%d" % b, "abu"], ["rg%d" % b])
-        if t == 0:
-            tt(T.oo[:, 32:32 + KB], T.abi[:, 0:KB], T.abi[:, KB:2 * KB], A.subtract, ["ai", "bi"], ["dd"])
-            act(T.ownb[:, 16:32], T.jw[:, 0:16], F.Identity, ["jw"], ["dump"], scale=4.0, bias=320.0)
-            nobody()
-            whole()
+        ts(T.abi[:, 0:KB], T.pi[:, 0:KB], 10, None, A.arith_shift_right, None, ["pi"], ["ai"])
+        cp(T.abu[:, KB:2 * KB], T.abi[:, KB:2 * KB], ["bi"], ["bu"])
+        slot(7)
+        act(T.dtile[:, 0:4 * K:4], T.sg[:].indirect(T.abu[:, 0:KB]), F.Copy, ["sg", "au"], ["dt0"])
+        for b in (2, 3, 0, 1):
+            first(b)
+        cp(T.dtile[:, 1:4 * K:4], T.sg[:].indirect(T.abu[:, KB:2 * KB]), ["sg", "bu"], ["dt1"])
+        tt(T.oo[:, 32:32 + KB], T.abi[:, 0:KB], T.abi[:, KB:2 * KB], A.subtract, ["ai", "bi"], ["dd"])
         quant("dq", 0, K, T.dtile[:], ["dt0", "dt1"])
         mm(7, "gq", 128, "dq", K, extra=["gq2"])
         mm(1, "gq", 256, "dq", K, extra=["gq2"])
-        diff(0)
+        diff(2)
+        if t == 0:
+            resets(range(0, 2))
+            act(T.ownb[:, 16:32], T.jw[:, 0:16], F.Identity, ["jw"], ["dump"], scale=4.0, bias=320.0)
         scan(T.pa[:, 0:K], ps(7, 0, K), T.kmid[:], -MID, A.max, A.add, ["ps7", "kmid"], ["pa"])
         scan(T.pb[:, 0:K], ps(1, 0, K), T.kq[:], -MID, A.max, A.add, ["ps1", "kq"], ["pb"])
-        diff(1)
-        tt(T.fi[:, 0:KB], T.pa[:, 15:K:16], T.pb[:, 15:K:16], A.mult, ["pa", "pb"], ["fi"])
-        diff(2)
-        ts(T.fi[:, 16:16 + KB], T.fi[:, 0:KB], 7, 1, A.arith_shift_right, A.bitwise_and, ["fi"], ["fj"])
         diff(3)
-        cp(T.su[:, 16:16 + KB], T.fi[:, 16:16 + KB], ["fj"], ["fu"])
+        turn(2)
+        turn(3)
+        tt(T.fi[:, 0:KB], T.pa[:, 15:K:16], T.pb[:, 15:K:16], A.mult, ["pa", "pb"], ["fi"])
+        diff(0)
+        ts(T.fi[:, 16:16 + KB], T.fi[:, 0:KB], 7, 1, A.arith_shift_right, A.bitwise_and, ["fi"], ["fj"])
+        diff(1)
+        tt(T.oo[:, 64:64 + KB], T.fi[:, 16:16 + KB], T.jw[:, 64:64 + KB], A.add, ["fj", "jw2"], ["f2"])
         tt(T.oo[:, 48:48 + KB], T.fi[:, 16:16 + KB], T.oo[:, 32:32 + KB], A.mult, ["fj", "dd"], ["ed"])
-        pack(0)
+        if t == 0:
+            resets(range(2, 3))
+        cp(T.su[:, 16:16 + KB], T.oo[:, 64:64 + KB], ["f2"], ["fu"])
         tt(T.lr[:, 0:KB], T.abi[:, 0:KB], T.oo[:, 48:48 + KB], A.subtract, ["ai", "ed"], ["lf"])
-        tt(T.lr[:, KB:2 * KB], T.abi[:, KB:2 * KB], T.oo[:, 48:48 + KB], A.add, ["bi", "ed"], ["rf"])
-        pack(1)
-        cp(T.lru[:, 0:2 * KB], T.lr[:, 0:2 * KB], ["lf", "rf"], ["lru"])
-        act(T.ownb[:, 0:KB], T.lr[:, 0:KB], F.Identity, ["lf"], ["ownb"], bias=-144.0)
-        act(T.rowf[:], T.iota[:].indirect(T.lru[:, 0:KB]), F.Identity, ["iota", "lru"], ["rowf"], bias=-144.0)
         if last:
-            act(T.r1[:], T.iota[:].indirect(T.lru[:, 0:2 * KB]), F.Copy, ["iota", "lru"], ["r1"])
+            tt(T.lr[:, KB:2 * KB], T.abi[:, KB:2 * KB], T.oo[:, 48:48 + KB], A.add, ["bi", "ed"], ["rf"])
+        if t == 0:
+            fill(T.lr[:, KB:16], 0.0, ["rf"])
+            cp(T.endu[:, 0:1], T.qf[:, 4:5], ["e2"], ["endu"])
         pack(2)
+        pack(0)
+        n = 2 * KB if last else KB
+        cp(T.lru[:, 0:n], T.lr[:, 0:n], ["lf", "rf"], ["lru"])
+        pack(1)
         pack(3)
+        act(T.rowf[:], T.iota[:].indirect(T.lru[:, 0:KB]), F.Identity, ["iota", "lru"], ["rowf"], bias=-144.0)
+        ts(T.ownb[:, 0:KB], T.lr[:, 0:KB], -144.0, None, A.add, None, ["lf"], ["ownb"])
+        if t == 0:
+            resets(range(3, KB))
         quant("mq", 0, K, T.mt[:], ["mt0", "mt1", "mt2", "mt3"])
         need("t", ("w%d" % t, _arrivals(T, topo, rank, t)))
+        left(0)
         for b in range(4):
             mm(2 + b, "wl%d" % t, 128 * b, "mq", K)
             act(T.ht[:, b:4 * K:4], ps(2 + b, 0, K), F.Copy, ["ps%d" % (2 + b)], ["ht%d" % b], scale=0.03125)
-        for b in (2, 3):
-            mm(b, "eq", 128 * b, "xq", C)
+        for b in (1, 2, 3):
+            left(b)
         if last:
-            act(T.r2[:], T.r1[:].indirect(T.revu[:, 0:2 * KB]), F.Copy, ["r1", "rev0", "rev1"], ["r2"])
-            dma("y", T.ol[:], T.r2[0:128:16, :], ["r2"], [])
+            act(T.r1[:], T.iota[:].indirect(T.lru[:, 0:2 * KB]), F.Copy, ["iota", "lru"], ["r1"])
         for c in range(KB):
             repeats(c)
         repeated(0, 6)
         repeated(6, KB)
-        tt(T.oo[:, 0:16], T.fl[:].indirect(T.endu[:, 0:1]), T.lr[:, 0:16], A.max, ["fl0", "fl6", "endu", "lf", "rf"], ["o1"])
         quant("rq", 0, K, T.ht[:], ["ht0", "ht1", "ht2", "ht3"])
         for b in range(4):
-            bank = (0, 1, 6, 7)[b]
-            mm(bank, "eq", 128 * b, "rq", K)
-            act(T.dh[:, DW * b:DW * b + K], ps(bank, 0, K), F.Copy, ["ps%d" % bank], ["dh%d" % b])
+            mm(DB[b], "eq", 128 * b, "rq", K)
+        if last:
+            act(T.r2[:], T.r1[:].indirect(T.revu[:, 0:2 * KB]), F.Copy, ["r1", "rev0", "rev1"], ["r2"])
+            dma("y", T.ol[:], T.r2[0:128:16, :], ["r2"], [])
+        tt(T.oo[:, 0:16], T.fl[:].indirect(T.endu[:, 0:1]), T.lr[:, 0:16], A.max, ["fl0", "fl6", "endu", "lf", "rf"], ["o1"])
         cp(T.su[:, 0:KB], T.oo[:, 0:KB], ["o1"], ["su"])
-        cp(T.who[:].indirect(T.su[:, 0:KB]), T.iota[:, 0:K], ["su", "iota"], ["who"])
+        renew(0)
+        cp(T.who[:].indirect(T.su[:, 0:KB]), T.iota[:, C - PW // 2:PW // 2], ["su", "iota"], ["who"])
+        renew(1)
         scan(T.whs[:], T.who[:, 0:C], T.klow[:], -LOW, A.max, A.add, ["who", "klow"], ["whs"])
-        ts(T.wu[:, 0:CB], T.whs[:, 15:C:16], LOW, None, A.add, None, ["whs"], ["wu"])
-        for b in (2, 3):
-            act(T.gd[:, C * (b - 2):C * (b - 1)], T.dh[:, DW * b:DW * b + K + 1].indirect(T.wu[:, 0:CB]), F.Copy,
-                ["dh%d" % b, "dhz", "wu"], ["gd%d" % b])
-        for b in (0, 1):
-            tt(T.xt[:, b:4 * C:4], T.dh[:, DW * b:DW * b + K + 1].indirect(T.wu[:, 0:CB]), T.tp[:, C * b:C * b + C], A.add,
-               ["dh%d" % b, "dhz", "wu", "tp"], ["xt%d" % b])
-        for b in (2, 3):
-            tt(T.xt[:, b:4 * C:4], ps(b, 0, C), T.gd[:, C * (b - 2):C * (b - 1)], A.add, ["ps%d" % b, "gd%d" % b],
-               ["xt%d" % b])
+        renew(2)
+        ts(T.wu[:, 0:CB], T.whs[:, 15:C:16], LOW + PW // 2, None, A.add, None, ["whs"], ["wu"])
+        renew(3)
+        for b in (1, 2):
+            act(T.xt[:, b:4 * C:4], held(b, PW).indirect(T.wu[:, 0:CB]), F.Copy, ["th%d" % b, "new%d" % b, "wu"],
+                ["xt%d" % b])
+        for b in (0, 3):
+            cp(T.xt[:, b:4 * C:4], held(b, PW).indirect(T.wu[:, 0:CB]), ["th%d" % b, "new%d" % b, "wu"], ["xt%d" % b])
 
     quant("xq", 0, C, T.xt[:], XT)
     mm(0, "vq", 0, "xq", H)

from concourse.bass import DstId, RemoteDMATransfer
from concourse.mybir import dt, AluOpType, ActivationFunctionType

C, K, R = 288, 160, 3
CB, KB = C // 16, K // 16
H = C // 2
NS = 2
BIG = 2.0 ** 96
TINY = 2.0 ** -120
LIFT, MID, LOW = 2.0 ** 20, 2.0 ** 12, 512.0
TW = [288, 224, 160, 160]
LO = 128
SEG = [176 * c - 8 * c * c for c in range(KB + 1)]
PW = C + K
RISE = (1.0 / 32, 0.5, 8.0, 128.0)
DB = (0, 1, 6, 7)
Q8, U8, BF, F32, I32, U16 = "float8_e4m3fn_x4", "uint8", "bfloat16", "float32", "int32", "uint16"

SCRATCH = {}


def _sb(name, n, d):
    SCRATCH[name] = ("sbuf", [128, n], d)


for _n, _w in (("wq", 512), ("hq", 128), ("wl0", 512), ("wl1", 512), ("wl2", 512), ("xq", C), ("uq", 128), ("ub", 128),
               ("vq", 128), ("eq", 512), ("gq", 384), ("zq", 128), ("dq", K), ("mq", K), ("rq", K),
               ("cq0", C), ("cq1", C), ("cq2", C), ("cq3", C)):
    _sb(_n, _w, Q8)
    _sb(_n + "s", _w, U8)
for _n, _w in (("xt", 4 * C), ("ut", 512), ("vt", 512), ("et", 2048), ("gt", 1536), ("ones", 512), ("zt", 640),
               ("srow", H), ("m01", H), ("m1", H), ("cdr", C), ("rst", H), ("sg", C), ("th", 4 * PW), ("sr", NS * C),
               ("pm", 2 * K), ("two", 4 * K), ("tl", 4 * K), ("junk", 2448), ("cd", C), ("dtile", 4 * K), ("rg", 6 * K),
               ("mt", 4 * K), ("ht", 4 * K), ("rowf", K), ("ownb", 32), ("ee", 960), ("dr", 960),
               ("fl", 960), ("who", 960), ("kbig", C), ("klow", C), ("kmid", K)):
    _sb(_n, _w, BF)
for _t in range(4):
    _sb("ct%d" % _t, 4 * TW[_t], BF)
for _n, _w in (("iota", C), ("lrow", C), ("lm", C), ("bm", C), ("lat", C), ("srt", C), ("pa", C), ("pb", C),
               ("pw", C), ("qf", 8), ("col", 16), ("jw", 96), ("blk", 32), ("rows", 32), ("zz", 96),
               ("lr", 32), ("oo", 96), ("r1", 2 * K), ("r2", 2 * K), ("yt", C), ("whs", C), ("kcol", C), ("kq", K)):
    _sb(_n, _w, F32)
for _n, _w in (("li", CB), ("mi", CB), ("pi", 16), ("abi", 32), ("fi", 32), ("ci", 16), ("gi", 32)):
    _sb(_n, _w, I32)
for _n, _w in (("lu", 32), ("mu", 32), ("pu", 16), ("qu", 32), ("gu", 32), ("ru", 32), ("abu", 32), ("lru", 32),
               ("endu", 16), ("su", 32), ("wu", 32), ("revu", 32)):
    _sb(_n, _w, U16)
for _b in range(8):
    SCRATCH["ps%d" % _b] = ("psum", [128, 512], F32)

NDMA = 60
SEMAPHORES = ["cv", "cs", "ct", "cg", "hin", "hout", "w0", "w1", "w2"] + ["d%d" % _i for _i in range(NDMA)]


def _bits(engines):
    m = 0
    for e in engines:
        m |= 1 << e
    return m


def _helpers(T, topo, r):
    n = len(T.cores)
    home = T.cores[r]
    return [c for c in topo.cores_of(home)
            if c != home and all(topo.may_write(c, T.cores[(r - 1 - t) % n]) for t in range(R))][:4]


def _arrivals(T, topo, r, t):
    e = (r + 1 + t) % len(T.cores)
    return sum(2 * len(topo.engines(h, T.cores[r])) for h in _helpers(T, topo, e))


def helper_program(g, core, T, topo, r, b):
    n = len(T.cores)
    share = len(topo.engines(T.cores[r], core)) // 4
    g.wait_ge(T.sem.hin, 2 * share)
    sent = 0
    for t in range(R):
        dst = T.cores[(r - 1 - t) % n]
        rid, pid = topo.addr(dst, core)
        mask = topo.mask(core, dst)
        sem = T.sem["w%d" % t]
        g.remote_dma(T["wl%d" % t][:, 128 * b:128 * b + 128].bitcast(dt.uint8), T.hq[:].bitcast(dt.uint8), sem,
                     T.sem.hout, pid, rid, mask)
        g.remote_dma(T["wl%ds" % t][:, 128 * b:128 * b + 128], T.hqs[:], sem, T.sem.hout, pid, rid, mask)
        sent += 2 * len(topo.engines(core, dst))
    g.wait_ge(T.sem.hout, sent)


def rank_program(g, core, T, topo):
    rank = T.rank_of(core)
    if rank is None:
        for r in range(len(T.cores)):
            hs = _helpers(T, topo, r)
            if core in hs:
                helper_program(g, core, T, topo, r, hs.index(core))
        return

    A, F = AluOpType, ActivationFunctionType
    V, S, PE, Y = g.vector, g.scalar, g.tensor, g.sync
    queue = {"v": V, "s": S, "t": PE, "g": g, "y": Y}
    count = {"v": 0, "s": 0, "t": 0, "g": 0}
    waited = {q: {} for q in queue}
    wrote, read = {}, {}
    ndma = [0]

    def need(q, tok):
        sem, n = tok[0], tok[1]
        if waited[q].get(sem, 0) < n:
            queue[q].wait_ge(T.sem[sem], n)
            waited[q][sem] = n

    def order(q, r, w):
        toks = []
        for k in r:
            toks += wrote.get(k, [])
            if k.startswith("ps"):
                toks += [x for x in read.get(k, []) if x[2] != q]
        for k in w:
            toks += wrote.get(k, []) + read.get(k, [])
        if q == "t":
            toks = [x for x in toks if x[2] != "t"]
        best = {}
        for x in toks:
            best[x[0]] = max(best.get(x[0], 0), x[1])
        for sem in best:
            need(q, (sem, best[sem]))

    def note(tok, r, w):
        for k in r:
            read.setdefault(k, []).append(tok)
        for k in w:
            wrote[k] = [tok]
            read[k] = []

    def op(q, fn, r, w):
        order(q, r, w)
        count[q] += 1
        fn().then_inc(T.sem["c" + q], 1)
        note(("c" + q, count[q], q), r, w)

    def dma(q, out, in_, r, w):
        order(q, r, w)
        sem = "d%d" % ndma[0]
        ndma[0] += 1
        queue[q].dma_start(out, in_).then_inc(T.sem[sem], 16)
        note((sem, 16, "dma"), r, w)

    def ts(out, in0, s1, s2, o0, o1, r, w):
        if o1 is None:
            op("v", lambda: V.tensor_scalar(out, in0, s1, None, o0), r, w)
        else:
            op("v", lambda: V.tensor_scalar(out, in0, s1, s2, o0, o1), r, w)

    def tt(out, a, b, o, r, w):
        op("v", lambda: V.tensor_tensor(out, a, b, o), r, w)

    def cp(out, in_, r, w):
        op("v", lambda: V.tensor_copy(out, in_), r, w)

    def fill(out, c, w):
        op("v", lambda: V.memset(out, c), [], w)

    def iota(out, pattern, base, w):
        op("g", lambda: g.iota(out, pattern, base, 0, allow_small_or_imprecise_dtypes=True), [], w)

    def scan(out, d0, d1, init, o0, o1, r, w):
        op("v", lambda: V.tensor_tensor_scan(out, d0, d1, init, o0, o1), r, w)

    def quant(name, a, b, tile, r, w=None):
        op("v", lambda: V.quantize_mx(T[name][:, a:b], T[name + "s"][:, a:b], tile), r, [w or name])

    def act(out, in_, func, r, w, **kw):
        op("s", lambda: S.activation(out, in_, func, **kw), r, w)

    def mm(bank, wname, w0, xname, n, start=True, stop=True, extra=(), x0=0):
        op("t", lambda: PE.matmul_mx(T["ps%d" % bank][:, 0:n], T[wname][:, w0:w0 + 128], T[wname + "s"][:, w0:w0 + 128],
                                     T[xname][:, x0:x0 + n], T[xname + "s"][:, x0:x0 + n], start, stop),
           [wname, xname] + list(extra), ["ps%d" % bank])

    def ps(bank, a, b):
        return T["ps%d" % bank][:, a:b]

    def weights():
        for base, ws in ((0, RISE), (4, RISE[::-1])):
            act(T.col[:, base:base + 1], T.m01[:, 1:2], F.Copy, ["m01"], ["col%d" % base], scale=ws[0])
        for i in range(1, 4):
            for base, ws in ((0, RISE), (4, RISE[::-1])):
                act(T.col[:, base + i:base + i + 1], T.m01[:, 1 + i:2 + i], F.Identity, ["m01", "col%d" % (base + i - 1)],
                    ["col%d" % (base + i)], scale=ws[i], bias=T.col[:, base + i - 1:base + i])
        act(T.col[:, 8:9], T.col[:, 3:4], F.Copy, ["col3", "gb"], ["col8"], scale=T.blk[:, 16:17])
        act(T.col[:, 10:11], T.col[:, 7:8], F.Copy, ["col7"], ["col10"], scale=-1.0)
        act(T.col[:, 9:10], T.col[:, 8:9], F.Copy, ["col8"], ["col9"], scale=-1.0)

    def tiles():
        act(T.gt[:, 1024:1536:4], T.gt[:, 0:512:4], F.Copy, ["gt0", "col10", "gz2"], ["gt2a"], scale=T.col[:, 10:11])
        act(T.gt[:, 512:1024:4], T.ones[:, 0:128], F.Copy, ["ones", "col8", "gz1"], ["gt1a"], scale=T.col[:, 8:9])
        act(T.gt[:, 1025:1536:4], T.gt[:, 0:512:4], F.Copy, ["gt0", "col7", "gz2"], ["gt2b"], scale=T.col[:, 7:8])
        act(T.gt[:, 513:1024:4], T.ones[:, 0:128], F.Copy, ["ones", "col9", "gz1"], ["gt1b"], scale=T.col[:, 9:10])

    def planes():
        for b in (2, 3, 0, 1):
            mm(2 + b, "eq", 128 * b, "xq", C)

    def held(b, n=C):
        return T.th[:, PW * b:PW * b + n]

    def plane(b):
        act(held(b), ps(2 + b, 0, C), F.Copy, ["ps%d" % (2 + b)], ["th%d" % b])

    def first(b):
        act(T.rg[:, K * b:K * b + K], held(b).indirect(T.abu[:, 0:KB]), F.Copy, ["th%d" % b, "au"], ["rg%d" % b])

    def diff(b):
        out = T.rg[:, K * (4 + b):K * (5 + b)] if b < 2 else T.two[:, 2 * K * (b - 2) + 1:2 * K * (b - 1):2]
        tt(out, held(b).indirect(T.abu[:, KB:2 * KB]), T.rg[:, K * b:K * b + K], A.subtract,
           ["th%d" % b, "bu", "rg%d" % b], ["df%d" % b])

    def turn(b):
        act(T.two[:, 2 * K * (b - 2):2 * K * (b - 1):2], T.two[:, 2 * K * (b - 2) + 1:2 * K * (b - 1):2], F.Copy,
            ["df%d" % b], ["dn%d" % b], scale=-1.0)

    def pack(b):
        if b < 2:
            tt(T.mt[:, b:4 * K:4], T.pm[:].indirect(T.su[:, 16:16 + KB]), T.rg[:, K * (4 + b):K * (5 + b)], A.mult,
               ["pm0", "pm1", "fu", "df%d" % b], ["mt%d" % b])
        else:
            act(T.mt[:, b:4 * K:4], T.two[:, 2 * K * (b - 2):2 * K * (b - 1)].indirect(T.su[:, 16:16 + KB]), F.Copy,
                ["fu", "df%d" % b, "dn%d" % b], ["mt%d" % b], scale=0.5)

    def left(b):
        act(T.tl[:, K * b:K * b + K], held(b).indirect(T.lru[:, 0:KB]), F.Copy, ["th%d" % b, "lru"], ["tl%d" % b])

    def renew(b):
        tt(T.th[:, PW * b + C:PW * b + PW], ps(DB[b], 0, K), T.tl[:, K * b:K * b + K], A.add,
           ["ps%d" % DB[b], "tl%d" % b], ["new%d" % b])

    def repeats(c):
        ts(T.ee[:, SEG[c]:SEG[c] + K - 16 * c], T.rowf[:, 16 * c:K], T.ownb[:, c:c + 1], T.ownb[:, 16 + c:17 + c],
           A.is_equal, A.mult, ["rowf", "ownb", "dump", "eea", "eeb"], ["ee%d" % c])

    def repeated(c0, c1):
        scan(T.fl[:, SEG[c0]:SEG[c1]], T.dr[:, SEG[c0]:SEG[c1]], T.ee[:, SEG[c0]:SEG[c1]], 0.0, A.mult, A.max,
             ["ee%d" % c for c in range(c0, c1)] + ["dr%d" % c for c in range(c0, c1)], ["fl%d" % c0])

    def line(c):
        s = CB - c
        tau, e, a = min(s // 4, 3), s % 4, LO * (s // 16)
        return T["ct%d" % tau][:, 4 * a + e:4 * (a + 16 * c):4]

    def lines(tau):
        return ["c%d" % c for c in (range(CB - 4 * tau - 3, CB - 4 * tau + 1) if tau < 3 else range(1, 7))]

    def own(c):
        return T.lat[:, 16 * c + 15:16 * c + 16]

    def compare(c):
        ts(line(c), ps(0, 0, 16 * c), own(c), None, A.is_lt, None, ["ps0", "lat%d" % (16 * c // H)], ["c%d" % c])
        jo = 8 * c * (c - 1)
        act(T.junk[:, jo:jo + 16 * c], line(c), F.Copy, ["c%d" % c], ["junk%d" % c, "row%d" % c],
            accum_out=T.rows[:, c:c + 1])

    def sums(tau):
        quant("cq%d" % tau, 0, TW[tau], T["ct%d" % tau][:], lines(tau))
        extra = ["cqh%d" % tau, "cqi%d" % tau]
        if tau < 3:
            mm(7, "gq", 0, "cq%d" % tau, C - LO, tau == 0, tau == 2, extra=extra, x0=LO)
            mm(6, "gq", 0, "cq%d" % tau, LO, tau == 0, False)
        else:
            mm(6, "gq", 0, "cq3", LO, False, False)
            mm(6, "gq", 0, "cq3", LO, False, True, extra=extra, x0=LO)

    def terms(h):
        a, b = (0, LO // 16) if h == 0 else (LO // 16, CB)
        tt(T.kcol[:, 16 * a + 15:16 * b:16], T.zz[:, 32 + a:32 + b], T.rows[:, a:b], A.add,
           ["z2", "rowz"] + ["row%d" % c for c in range(max(a, 1), b)], ["kcol%d" % h])

    def places(h):
        a, b = (0, LO) if h == 0 else (LO, C)
        scan(T.pw[:, a:b], ps(6 + h, 0, b - a), T.kcol[:, a:b], -LIFT, A.max, A.add, ["ps%d" % (6 + h), "kcol%d" % h],
             ["pw%d" % h])

    def offsets(h):
        a, b = (0, LO // 16) if h == 0 else (LO // 16, CB)
        ts(T.ru[:, a:b], T.pw[:, 16 * a + 15:16 * b:16], LIFT, None, A.add, None, ["pw%d" % h], ["ru%d" % h])

    def spread(h):
        a, b = (0, LO // 16) if h == 0 else (LO // 16, CB)
        cp(T.srt[:].indirect(T.ru[:, a:b]), T.lm[:, 16 * a:16 * b], ["ru%d" % h, "lm"], ["srt"])

    XT = ["xt0", "xt1", "xt2", "xt3"]
    dma("s", T.ut[:], T.u[:], [], ["ut"])
    dma("y", T.xt[:], T.x[:], [], XT)
    dma("y", T.li[:], T.l[:], [], ["li"])
    dma("y", T.mi[:], T.m[:], [], ["mi"])
    dma("y", T.wq[:].bitcast(dt.uint8), T.wc[:], [], ["wq"])
    dma("y", T.wqs[:], T.ws[:], [], ["wqs"])

    q = T.qf[:, 0:1]
    fill(T.zt[:], 0.0, ["zt"])
    fill(T.ones[:], 1.0, ["ones"])
    op("g", lambda: g.iota(T.ci[:, 0:1], [[0, 1]], 0, 1), [], ["ci0"])
    iota(T.jw[:, 0:20], [[16, 20]], 0, ["jw"])
    iota(T.srow[:], [[0, H // 16], [1, 16]], 0, ["srow"])
    op("g", lambda: g.iota(T.gi[:], [[1, 8], [0, 4]], 0, 0), [], ["gi"])
    iota(T.iota[:], [[1, C]], 0, ["iota"])
    iota(T.cdr[:], [[0, C]], 256, ["cdr"])
    iota(T.cdr[:, 0:C:16], [[-16, CB]], H, ["cdr"])

    for t in range(4):
        n = (192, 192, 192, 448)[t]
        act(T["ct%d" % t][:, 4 * TW[t] - n:4 * TW[t]], T.zt[:, 0:n], F.Copy, ["zt"], lines(t))
    for b in range(4):
        dma("y", T.et[:, 512 * b:512 * b + 512], T.zt[:, 0:512], ["zt"], ["et%d" % b])
    quant("zq", 0, 128, T.zt[:, 0:512], ["zt"])
    for t in range(1, 4):
        n = C - TW[t]
        dma("y", T["cq%d" % t][:, C - n:C].bitcast(dt.uint8), T.zq[:, 0:n].bitcast(dt.uint8), ["zq"], ["cqh%d" % t])
        dma("y", T["cq%ds" % t][:, C - n:C], T.zqs[:, 0:n], ["zq"], ["cqi%d" % t])
    dma("y", T.gt[:, 512:1024], T.zt[:, 0:512], ["zt"], ["gz1"])
    dma("y", T.gt[:, 1024:1536], T.zt[:, 0:512], ["zt"], ["gz2"])
    dma("y", T.dtile[:], T.zt[:], ["zt"], ["dt0", "dt1"])
    dma("y", T.dr[:, 0:480], T.ones[:, 0:480], ["ones"], ["dra"])
    dma("y", T.dr[:, 480:960], T.ones[:, 0:480], ["ones"], ["drb"])
    dma("y", T.ee[:, 0:480], T.zt[:, 0:480], ["zt"], ["eea"])
    dma("y", T.ee[:, 480:960], T.zt[:, 0:480], ["zt"], ["eeb"])
    dma("y", T.vt[:], T.v[:], [], ["vt"])

    ts(T.ci[:, 1:2], T.ci[:, 0:1], 15, None, A.bitwise_and, None, ["ci0"], ["ci1"])
    cp(T.qf[:, 1:2], T.ci[:, 0:1], ["ci0"], ["p"])
    cp(T.pu[:, 0:8], T.jw[:, 0:8], ["jw"], ["pu"])
    fill(T.rows[:, 0:1], 0.0, ["rowz"])
    cp(q, T.ci[:, 1:2], ["ci1"], ["q"])
    ts(T.rst[:], T.srow[:], 2 * BIG, -BIG, A.mult, A.add, ["srow"], ["rst"])
    cp(T.gu[:], T.gi[:], ["gi"], ["gu"])
    ts(T.jw[:, 0:20], T.jw[:, 0:20], q, None, A.add, None, ["jw", "q"], ["jw"])
    ts(T.m01[:], T.srow[:], q, None, A.is_equal, None, ["srow", "q"], ["m01"])
    ts(T.zz[:, 0:16], T.srow[:, 0:16], q, -1.0, A.is_lt, A.mult, ["srow", "q"], ["z1"])
    ts(T.blk[:, 16:24], T.jw[:, 0:8], T.qf[:, 1:2], None, A.is_equal, None, ["jw", "p"], ["gb"])
    ts(T.qu[:, 0:CB], T.zt[:, 0:CB], q, None, A.add, None, ["zt", "q"], ["qu"])
    tt(T.blk[:, 0:16], T.zz[:, 0:16], T.m01[:, 0:16], A.add, ["z1", "m01"], ["kb"])
    ts(T.m1[:], T.m01[:], 2 * BIG, -BIG, A.mult, A.add, ["m01"], ["m1"])
    ts(T.blk[:, 15:16], T.blk[:, 15:16], -2.0, None, A.add, None, ["kb"], ["kb"])
    act(T.gt[:, 0:512], T.blk[:, 16:24].indirect(T.gu[:]), F.Copy, ["gb", "gu"], ["gt0"], scale=-1.0)

    quant("uq", 0, 128, T.ut[:], ["ut"])
    ts(T.qf[:, 2:3], q, 1.0, float(KB), A.add, A.min, ["q"], ["e0"])
    cp(T.ub[:].bitcast(dt.uint32), T.uq[:].bitcast(dt.uint32).indirect(T.pu[:, 0:8]), ["uq", "pu"], ["ub"])
    act(T.ubs[:], T.uqs[:].indirect(T.pu[:, 0:8]), F.Copy, ["uq", "pu"], ["ubs"])
    act(T.kcol[:], T.blk[:, 0:16].indirect(T.qu[:, 0:CB]), F.Copy, ["kb", "qu"], ["kcol0", "kcol1"], scale=LIFT)

    hs = _helpers(T, topo, rank)
    eng = topo.engines(core, hs[0])
    share = len(eng) // 4
    for name, land in (("wq", "hq"), ("wqs", "hqs")):
        order("g", [name], [])
        trs = []
        for b, h in enumerate(hs):
            rid, pid = topo.addr(h, core)
            src, dst = T[name][:, 128 * b:128 * b + 128], T[land][:]
            if name == "wq":
                src, dst = src.bitcast(dt.uint8), dst.bitcast(dt.uint8)
            trs.append(RemoteDMATransfer(dst_ids=[DstId(rid=rid, pnc=pid)],
                                         dma_engine_mask=_bits(eng[share * b:share * b + share]),
                                         remote_sem=T.sem.hin, src=src, dst=dst))
        g.remote_dma_fused(trs, local_sem=T.sem.hout)
    for b in (2, 3, 0, 1):
        op("g", lambda: g.affine_select(T.et[:, 512 * b + b:512 * b + 512:4], T.ones[:, 0:128], [[-1, 128]], A.is_equal,
                                        0.0, 0, 1), ["ones"], ["et%d" % b])

    def resets(cs):
        for c in cs:
            ts(T.dr[:, SEG[c] + 1:SEG[c] + 17], T.m01[:, 0:16], -1.0, 1.0, A.mult, A.add, ["m01", "dra", "drb"],
               ["dr%d" % c])

    later = [
        lambda: ts(T.kbig[:, 0:K], T.kcol[:, 0:K], 1.0, None, A.mult, None, ["kcol0", "kcol1"], ["kbig"]),
        lambda: tt(T.lm[:], T.iota[:].indirect(T.mu[:, 0:CB]), T.lrow[:], A.add, ["iota", "mu", "lrow"], ["lm"]),
        lambda: ts(T.kmid[:], T.kbig[:, 0:K], MID / LIFT, None, A.mult, None, ["kbig"], ["kmid"]),
        lambda: ts(T.kq[:], T.kbig[:, 0:K], MID / LIFT, None, A.mult, None, ["kbig"], ["kq"]),
        lambda: (ts(T.kq[:, 15:K:16], T.kq[:, 15:K:16], -8.0 / MID, None, A.add, None, ["kq"], ["kq"]),
                 ts(T.qf[:, 3:4], T.qf[:, 2:3], -8.0, 176.0, A.mult, A.add, ["e0"], ["e1"])),
        lambda: (fill(T.pm[:, 0:2 * K:2], -0.5, ["pm0"]), fill(T.pm[:, 1:2 * K:2], 0.5, ["pm1"])),
        lambda: (ts(T.qf[:, 4:5], T.qf[:, 3:4], T.qf[:, 2:3], 1.0, A.mult, A.subtract, ["e0", "e1"], ["e2"]),
                 ts(T.jw[:, 64:64 + KB], T.jw[:, 0:KB], 2.0, None, A.mult, None, ["jw"], ["jw2"])),
        lambda: quant("gq", 128, 384, T.gt[:, 512:1536], ["gt1a", "gt1b", "gt2a", "gt2b"], "gq2"),
    ]

    for t in range(R):
        last = t == R - 1

        def slot(i):
            if t == 0:
                later[i]()

        quant("xq", 0, C, T.xt[:], XT)
        mm(0, "ub", 0, "xq", C, extra=["ubs"])
        mm(7, "ub", 0, "xq", C, extra=["ubs"])
        mm(1, "uq", 0, "xq", C)
        if t == 0:
            quant("gq", 0, 128, T.gt[:, 0:512], ["gt0"])
            cp(T.lu[:, 0:CB], T.li[:], ["li"], ["lu"])
            cp(T.mu[:, 0:CB], T.mi[:], ["mi"], ["mu"])
            ts(T.qf[:, 5:6], T.blk[:, 15:16], LIFT, float(C - 16 - H), A.mult, A.add, ["kb"], ["k0"])
        else:
            planes()
        iota(T.who[:, 0:C], [[1, C]], -PW // 2, ["who"])
        if t == 1:
            quant("vq", 0, 128, T.vt[:], ["vt"])
        if last:
            ts(T.revu[:, 0:KB], T.jw[:, 0:KB], -1.0, float(K - 1), A.mult, A.add, ["jw"], ["rev0"])
            ts(T.revu[:, KB:2 * KB], T.jw[:, KB:2 * KB], -1.0, float(3 * K - 1), A.mult, A.add, ["jw"], ["rev1"])
        for h in (1, 0):
            tt(T.bm[:, H * h:H * h + H], ps(0, H * h, H * h + H), T.m1[:, 0:H], A.min, ["ps0", "m1"], ["bm%d" % h])
        for h in (1, 0):
            scan(T.lat[:, H * h:H * h + H], T.rst[:, 0:H], T.bm[:, H * h:H * h + H], -BIG, A.min, A.max,
                 ["rst", "bm%d" % h], ["lat%d" % h])
        if t == 0:
            act(T.klow[:], T.kcol[:], F.Copy, ["kcol0", "kcol1"], ["klow"], scale=LOW / LIFT)
        for i in range(NS):
            c = CB - 1 - i
            act(T.sr[:, C * i:C * i + 16 * c], ps(7, 0, 16 * c), F.Sign, ["ps7", "lat1"], ["sr%d" % c],
                scale=-1.0, bias=own(c))
        for i in range(NS):
            c = CB - 1 - i
            act(line(c), T.sr[:, C * i:C * i + 16 * c], F.Relu, ["sr%d" % c], ["c%d" % c, "row%d" % c],
                accum_out=T.rows[:, c:c + 1])
        compare(CB - 1 - NS)
        if t == 0:
            tt(T.qf[:, 6:7], T.qf[:, 5:6], q, A.add, ["k0", "q"], ["k1"])
        tt(T.ct0[:, 0:4 * C:4], ps(0, 0, C), T.lat[:], A.is_le, ["ps0", "lat0", "lat1"], ["c%d" % CB])
        for c in range(CB - 2 - NS, 0, -1):
            compare(c)
            if c == 13:
                scan(T.cd[:], T.cdr[:], T.ct0[:, 0:4 * C:4], 256.0, A.min, A.add, ["cdr", "c%d" % CB], ["cd"])
            if c in (11, 9, 5):
                sums((11, 9, 5).index(c))
            if c == 9:
                act(T.zz[:, 32:32 + CB], T.cd[:, 15:C:16], F.Identity, ["cd", "k1"], ["z2"], bias=T.qf[:, 6:7])
            if c == 3:
                slot(0)
        if t == 0:
            act(T.lrow[:], T.iota[:].indirect(T.lu[:, 0:CB]), F.Copy, ["iota", "lu"], ["lrow"], scale=1024.0)
        terms(1)
        sums(3)
        if t == 0:
            quant("eq", 0, 512, T.et[:], ["et0", "et1", "et2", "et3"])
            planes()
        places(1)
        terms(0)
        slot(1)
        act(T.sg[:], ps(1, 0, C), F.Sign, ["ps1"], ["sg"], bias=-TINY)
        if t == 0:
            weights()
        for b in (2, 3):
            plane(b)
        if t == 0:
            tiles()
        for b in (0, 1):
            plane(b)
        offsets(1)
        places(0)
        spread(1)
        slot(2)
        offsets(0)
        slot(3)
        spread(0)
        slot(4)
        scan(T.pa[:, 0:K], T.srt[:, C - K:C], T.kbig[:, 0:K], -LIFT, A.max, A.add, ["srt", "kbig"], ["pa"])
        slot(5)
        ts(T.pi[:, 0:KB], T.pa[:, 15:K:16], LIFT, None, A.add, None, ["pa"], ["pi"])
        ts(T.abu[:, 0:KB], T.pa[:, 15:K:16], LIFT, 1.0 / 1024, A.add, A.mult, ["pa"], ["au"])
        slot(6)
        ts(T.abi[:, KB:2 * KB], T.pi[:, 0:KB], 1023, None, A.bitwise_and, None, ["pi"], ["bi"])
        ts(T.abi[:, 0:KB], T.pi[:, 0:KB], 10, None, A.arith_shift_right, None, ["pi"], ["ai"])
        cp(T.abu[:, KB:2 * KB], T.abi[:, KB:2 * KB], ["bi"], ["bu"])
        slot(7)
        act(T.dtile[:, 0:4 * K:4], T.sg[:].indirect(T.abu[:, 0:KB]), F.Copy, ["sg", "au"], ["dt0"])
        for b in (2, 3, 0, 1):
            first(b)
        cp(T.dtile[:, 1:4 * K:4], T.sg[:].indirect(T.abu[:, KB:2 * KB]), ["sg", "bu"], ["dt1"])
        tt(T.oo[:, 32:32 + KB], T.abi[:, 0:KB], T.abi[:, KB:2 * KB], A.subtract, ["ai", "bi"], ["dd"])
        quant("dq", 0, K, T.dtile[:], ["dt0", "dt1"])
        mm(7, "gq", 128, "dq", K, extra=["gq2"])
        mm(1, "gq", 256, "dq", K, extra=["gq2"])
        diff(2)
        if t == 0:
            resets(range(0, 2))
            act(T.ownb[:, 16:32], T.jw[:, 0:16], F.Identity, ["jw"], ["dump"], scale=4.0, bias=320.0)
        scan(T.pa[:, 0:K], ps(7, 0, K), T.kmid[:], -MID, A.max, A.add, ["ps7", "kmid"], ["pa"])
        scan(T.pb[:, 0:K], ps(1, 0, K), T.kq[:], -MID, A.max, A.add, ["ps1", "kq"], ["pb"])
        diff(3)
        turn(2)
        turn(3)
        tt(T.fi[:, 0:KB], T.pa[:, 15:K:16], T.pb[:, 15:K:16], A.mult, ["pa", "pb"], ["fi"])
        diff(0)
        ts(T.fi[:, 16:16 + KB], T.fi[:, 0:KB], 7, 1, A.arith_shift_right, A.bitwise_and, ["fi"], ["fj"])
        diff(1)
        tt(T.oo[:, 64:64 + KB], T.fi[:, 16:16 + KB], T.jw[:, 64:64 + KB], A.add, ["fj", "jw2"], ["f2"])
        tt(T.oo[:, 48:48 + KB], T.fi[:, 16:16 + KB], T.oo[:, 32:32 + KB], A.mult, ["fj", "dd"], ["ed"])
        if t == 0:
            resets(range(2, 3))
        cp(T.su[:, 16:16 + KB], T.oo[:, 64:64 + KB], ["f2"], ["fu"])
        tt(T.lr[:, 0:KB], T.abi[:, 0:KB], T.oo[:, 48:48 + KB], A.subtract, ["ai", "ed"], ["lf"])
        if last:
            tt(T.lr[:, KB:2 * KB], T.abi[:, KB:2 * KB], T.oo[:, 48:48 + KB], A.add, ["bi", "ed"], ["rf"])
        if t == 0:
            fill(T.lr[:, KB:16], 0.0, ["rf"])
            cp(T.endu[:, 0:1], T.qf[:, 4:5], ["e2"], ["endu"])
        pack(2)
        pack(0)
        n = 2 * KB if last else KB
        cp(T.lru[:, 0:n], T.lr[:, 0:n], ["lf", "rf"], ["lru"])
        pack(1)
        pack(3)
        act(T.rowf[:], T.iota[:].indirect(T.lru[:, 0:KB]), F.Identity, ["iota", "lru"], ["rowf"], bias=-144.0)
        ts(T.ownb[:, 0:KB], T.lr[:, 0:KB], -144.0, None, A.add, None, ["lf"], ["ownb"])
        if t == 0:
            resets(range(3, KB))
        quant("mq", 0, K, T.mt[:], ["mt0", "mt1", "mt2", "mt3"])
        need("t", ("w%d" % t, _arrivals(T, topo, rank, t)))
        left(0)
        for b in range(4):
            mm(2 + b, "wl%d" % t, 128 * b, "mq", K)
            act(T.ht[:, b:4 * K:4], ps(2 + b, 0, K), F.Copy, ["ps%d" % (2 + b)], ["ht%d" % b], scale=0.03125)
        for b in (1, 2, 3):
            left(b)
        if last:
            act(T.r1[:], T.iota[:].indirect(T.lru[:, 0:2 * KB]), F.Copy, ["iota", "lru"], ["r1"])
        for c in range(KB):
            repeats(c)
        repeated(0, 6)
        repeated(6, KB)
        quant("rq", 0, K, T.ht[:], ["ht0", "ht1", "ht2", "ht3"])
        for b in range(4):
            mm(DB[b], "eq", 128 * b, "rq", K)
        if last:
            act(T.r2[:], T.r1[:].indirect(T.revu[:, 0:2 * KB]), F.Copy, ["r1", "rev0", "rev1"], ["r2"])
            dma("y", T.ol[:], T.r2[0:128:16, :], ["r2"], [])
        tt(T.oo[:, 0:16], T.fl[:].indirect(T.endu[:, 0:1]), T.lr[:, 0:16], A.max, ["fl0", "fl6", "endu", "lf", "rf"], ["o1"])
        cp(T.su[:, 0:KB], T.oo[:, 0:KB], ["o1"], ["su"])
        renew(0)
        cp(T.who[:].indirect(T.su[:, 0:KB]), T.iota[:, C - PW // 2:PW // 2], ["su", "iota"], ["who"])
        renew(1)
        scan(T.whs[:], T.who[:, 0:C], T.klow[:], -LOW, A.max, A.add, ["who", "klow"], ["whs"])
        renew(2)
        ts(T.wu[:, 0:CB], T.whs[:, 15:C:16], LOW + PW // 2, None, A.add, None, ["whs"], ["wu"])
        renew(3)
        for b in (1, 2):
            act(T.xt[:, b:4 * C:4], held(b, PW).indirect(T.wu[:, 0:CB]), F.Copy, ["th%d" % b, "new%d" % b, "wu"],
                ["xt%d" % b])
        for b in (0, 3):
            cp(T.xt[:, b:4 * C:4], held(b, PW).indirect(T.wu[:, 0:CB]), ["th%d" % b, "new%d" % b, "wu"], ["xt%d" % b])

    quant("xq", 0, C, T.xt[:], XT)
    mm(0, "vq", 0, "xq", H)
    mm(1, "vq", 0, "xq", H, x0=H)
    dma("y", T.oc[:], T.xq[:].bitcast(dt.uint8), ["xq"], [])
    for k in range(4):
        dma("y" if k % 2 else "s", T.osc[4 * k:4 * k + 4, :], T.xqs[32 * k:32 * k + 4, :], ["xq"], [])
    cp(T.yt[:, 0:H], ps(0, 0, H), ["ps0"], ["yt0"])
    act(T.yt[:, H:C], ps(1, 0, H), F.Copy, ["ps1"], ["yt1"])
    dma("y", T.y[:, 0:H], T.yt[:, 0:H], ["yt0"], [])
    dma("s", T.y[:, H:C], T.yt[:, H:C], ["yt1"], [])

    g.wait_ge(T.sem.hout, 8 * share)
    need("g", ("cg", count["g"]))
    need("t", ("ct", count["t"]))
    need("v", ("cv", count["v"]))
    need("s", ("cs", count["s"]))
    for i in range(ndma[0]):
        if not any(waited[x].get("d%d" % i, 0) for x in waited):
            need("g", ("d%d" % i, 16))
